import numpy as np, ml_dtypes
CORES = [5,29,101,125,133,157,229,253]
N = 8
import mx_ref
BF = ml_dtypes.bfloat16
def entries(a):
    return np.ascontiguousarray(a.T).reshape(-1)
def table(e):
    return np.ascontiguousarray(np.reshape(e, (-1, 16)).T).astype(np.int32)
def pick(q, e):
    c = np.concatenate([q[0].reshape(128, -1, 4), np.zeros((128, 1, 4), np.uint8)], axis=1); s = np.concatenate([q[1], np.ones((16, 1), np.uint8)], axis=1)
    return (np.ascontiguousarray(c[:, e].reshape(128, -1)), np.ascontiguousarray(s[:, e]))
def join(*qs):
    return (np.concatenate([q[0] for q in qs], axis=1), np.concatenate([q[1] for q in qs], axis=1))
def put(q, e, v):
    c, s = q[0].reshape(128, -1, 4).copy(), q[1].copy(); c[:, e] = v[0].reshape(128, -1, 4); s[:, e] = v[1]
    return (c.reshape(128, -1), s)
def pk(c, s):
    return (np.ascontiguousarray(c), mx_ref.live(s))
def emit(q):
    return q[0], q[1]
def decode(q):
    o = []
    for b in range(4):
        e = np.zeros((128, 128, 4), np.float32); e[np.arange(128), np.arange(128), b] = 1
        o.append(mx_ref.matmul(mx_ref.quantize(e.reshape(128, 512).astype(BF)), q))
    return np.stack(o, axis=2).reshape(128, -1)
def cut(t, i, w=512):
    return t[:, w * i:w * i + w]
def f(rng, *shape):
    return mx_ref.flush((rng.standard_normal(shape, dtype=np.float32) * np.exp2(rng.integers(-2, 3, shape[:-1] + (1,)))).astype(BF))
def wide(rng, *shape, cols=0):
    v = rng.standard_normal(shape, dtype=np.float32) * np.exp2(rng.integers(-12, 13, shape)).astype(np.float32)
    if cols: v *= np.repeat(np.exp2(rng.integers(-cols, cols + 1, shape[:-2] + (1, shape[-1] // 4))) * (rng.random(shape[:-2] + (1, shape[-1] // 4)) > 0.0625), 4, axis=-1).astype(np.float32)
    return mx_ref.flush(v.astype(BF))
P, S, K, R, B, M, O = 128, 16, 16, 3, 24, 4, 3
def big(v):
    v = np.array(v).astype(np.float32)
    v[np.abs(v) < np.float32(2.0 ** -16)] = 0
    return v.astype(BF)
def link(adj, a, b):
    a, b = int(a), int(b)
    if a != b and len(adj[a]) < M and len(adj[b]) < M and b not in adj[a]:
        adj[a].append(b)
        adj[b].append(a)
def inner(rng, adj, e):
    for t in range(2 * M):
        a = rng.permutation(e)
        for i in range(0, a.size - 1, 2): link(adj, a[i], a[i + 1])
def across(rng, adj, ranks):
    for r in ranks:
        for q in ranks:
            if r < q:
                a, c = P * r + rng.permutation(P), P * q + rng.permutation(P)
                n = int(rng.integers(B // 2, B + 1))
                for i in range(n):
                    link(adj, a[i], c[i])
                    if i % 3 == 0: link(adj, a[i], c[(i + 1) % n])
def graph(rng):
    adj = [[] for a in range(N * P)]
    across(rng, adj, range(N))
    for r in range(N): inner(rng, adj, np.arange(P * r, P * r + P))
    return adj
def seeds(rng):
    return np.stack([rng.permutation(P)[:S] for r in range(N)])
def lists(rng, adj, s, late=False):
    at = np.argsort(rng.random((N * P, M)), axis=1)
    seed = np.zeros(N * P, bool)
    for r in range(N): seed[P * r + s[r]] = True
    n = np.full((N, M, P), -1)
    for a in range(N * P):
        k, e = at[a, :len(adj[a])], adj[a]
        if late: k, e = np.sort(k), sorted(e, key=lambda c: bool(seed[c]))
        for i, c in zip(k, e): n[a // P, i, a % P] = c
    return {"nb": np.stack([table(v.reshape(-1)) for v in n]), "sd": np.stack([table(v) for v in s])}
def plain(rng):
    return {"x": big(f(rng, N, 128, 4 * P)), "w": f(rng, N, 128, 512 * O)}
def setup_inputs(rng):
    return {**plain(rng), **lists(rng, graph(rng), seeds(rng))}
def setup_inputs_caps(rng):
    o = np.stack([rng.permutation(P) for r in range(N)])
    adj = [[] for a in range(N * P)]
    dense = int(rng.integers(0, N))
    for r in range(N):
        q = (r + 1) % N
        if r == dense:
            a = P * r + np.concatenate([o[r, S:S + K], o[r, K + B:2 * B]])
            c = P * q + np.concatenate([o[q, :S // 2], rng.permutation(np.concatenate([o[q, S // 2:S], o[q, S + K:K + B]]))])
            for i in range(B):
                for j in range(i - i % M, min(i - i % M + M, B)): link(adj, a[i], c[j])
        else:
            for i in range(K):
                link(adj, P * r + o[r, S + i], P * q + o[q, i])
                link(adj, P * r + o[r, S + i], P * q + o[q, S + K + i % (B - S)])
    for r in range(N): inner(rng, adj, P * r + o[r, S:])
    return {**plain(rng), **lists(rng, adj, o[:, :S])}
def setup_inputs_few(rng):
    adj, s, o, n, m = [[] for a in range(N * P)], seeds(rng), rng.permutation(N), K // 2 - 1, S // 2
    some, rest = int(o[1]), sorted(o[2:].tolist())
    ends = np.unique([0, 127, P - 1])
    s[some] = rng.permutation(np.setdiff1d(np.arange(P), ends))[:S]
    free, at, zero = rng.permutation(np.setdiff1d(np.arange(P), np.concatenate([s[some], ends]))), 0, []
    for i in range(K // 2):
        end = s[some, i]
        for t in range(1 + i % R):
            link(adj, P * some + end, P * some + free[at])
            end = free[at]
            at += 1
        if i < K // 4: zero.append(int(end))
    idle = np.sort(free[at:])
    lone = np.concatenate([ends, idle[:n - ends.size]])
    idle = rng.permutation(idle[n - ends.size:])
    for i in range(idle.size): link(adj, P * some + idle[i - 1], P * some + idle[i])
    for r in rest[:2]:
        g, e = rng.permutation(P // 8)[:n], P // 8 + rng.permutation(P // 8)[:m]
        s[r] = rng.permutation(np.setdiff1d(np.arange(P), np.concatenate([g, e])))[:S]
        high = rng.permutation(np.setdiff1d(np.arange(3 * P // 8, P), s[r]))
        for i in range(K): link(adj, P * r + s[r, i], P * r + high[i])
        for i in range(n):
            link(adj, P * r + s[r, i], P * r + g[i])
            link(adj, P * some + lone[i], P * r + g[i])
        for i in range(m):
            link(adj, P * r + s[r, n + i], P * r + e[i])
            link(adj, P * some + s[some, m + i], P * r + e[i])
    across(rng, adj, rest)
    for r in rest: inner(rng, adj, np.arange(P * r, P * r + P))
    sign = np.ones(N)
    sign[rest[::2]] = -0.75
    j = np.arange(P)
    v = f(rng, N, 128, 4 * P).astype(np.float32).reshape(N, 128, P, 4)
    v[:, :64] = 0
    for r in range(N):
        on = np.isin(j, s[r])
        v[r][64:96][:, ~on] = 0
        v[r][96:][:, on] = 0
        v[r, 0, :, 0] = 1024.0 * np.where(on, 1.0, sign[r])
        v[r, 40, :, 0] = np.where(on, rng.integers(1, 3, P), 0.125 * (8 * j // P))
    for r in rest[:2]: v[r, 40, s[r, n:n + m], 0] = 2.0
    v[some, 40, s[some, m:], 0] = 1.0
    v[some, 0, lone, 0] = 4096.0
    v[some][:, zero] = 0
    return {**plain(rng), "x": big(v.reshape(N, 128, 4 * P)), **lists(rng, adj, s)}
def setup_inputs_huge(rng):
    s = seeds(rng)
    v = rng.random((N, 128, P, 4), dtype=np.float32)
    for r in range(N):
        on = np.isin(np.arange(P), s[r])[None, :, None]
        u = ((0.7 + 0.85 * rng.random(P)) * (1 - 2 * (r % 2)))[None, :, None]
        v[r] = np.where(on, 1.7 + 0.28 * v[r], (0.8 + 0.45 * v[r]) * u)
    return {**plain(rng), "x": big((v * np.float32(2.0 ** 29)).reshape(N, 128, 4 * P)), **lists(rng, graph(rng), s)}
def setup_inputs_spread(rng):
    return {**setup_inputs(rng), "x": big(wide(rng, N, 128, 4 * P, cols=6))}
def setup_inputs_ties(rng):
    g = rng.integers(4, 8, (128, 3, 4)) * np.exp2(rng.integers(-2, 1, (128, 3, 4))) * rng.choice([-1.0, 1.0], (128, 3, 4)) * np.exp2(rng.integers(-2, 3, (128, 3, 1)))
    h = rng.integers(0, 3, (N, P))
    h[::2] = 0
    return {**plain(rng), "x": big(np.stack([g[:, h[r]].reshape(128, -1) for r in range(N)])), **lists(rng, graph(rng), seeds(rng), late=True)}
def check_inputs(d):
    b = []
    for k, low in (("x", 2.0 ** -16), ("w", 2.0 ** -30)):
        v = np.abs(d[k].astype(np.float32))
        if not (np.isfinite(v).all() and ((v == 0) | (v >= low) & (v <= 2.0 ** 30)).all()): b.append("a value of " + k)
    for r in range(N):
        e = entries(d["sd"][r])
        if e.min() < 0 or e.max() >= P or np.unique(e).size != S: b.append("sd")
    e = np.concatenate([entries(d["nb"][r]).reshape(M, P) for r in range(N)], axis=1).astype(np.int64)
    if e.min() < -1 or e.max() >= N * P: return b + ["nb"]
    k, j = np.nonzero(e >= 0)
    n = e[k, j]
    a, c = j * (N * P) + n, n * (N * P) + j
    if (n == j).any() or np.unique(a).size != a.size: b.append("nb names a place twice or itself")
    if not np.array_equal(np.sort(a), np.sort(c)): b.append("nb isn't symmetric")
    for r in range(N):
        for q in range(N):
            if q != r and np.count_nonzero((e[:, P * r:P * r + P] // P == q).any(axis=0)) > B: b.append("places with neighbours on one other rank")
    return b
def reference(x, w, nb, sd):
    first = join(*[mx_ref.quantize(np.ascontiguousarray(x[r])) for r in range(N)])
    now = first
    near = np.concatenate([entries(nb[r]).reshape(M, P) for r in range(N)], axis=1)
    parent = np.full(N * P, -1)
    fresh = np.concatenate([P * r + entries(sd[r]) for r in range(N)])
    parent[fresh] = fresh
    score = np.full((M, N * P), -np.inf, np.float32)
    for t in range(R):
        spot = np.full(N * P + 1, -1)
        spot[fresh] = np.arange(fresh.size)
        side = pick(now, np.concatenate([fresh, np.full(4 + -fresh.size % 4, -1)]))
        z = np.concatenate([mx_ref.matmul(pick(first, np.arange(i, i + 128)), side) for i in range(0, N * P, 128)])
        k, j = np.nonzero(spot[near] >= 0)
        score[k, j] = z[j, spot[near[k, j]]] + np.float32(0)
        best, at = score.max(axis=0), score.argmax(axis=0)
        chosen = []
        for r in range(N):
            mine = np.arange(P * r, P * r + P)
            c = mine[(parent[mine] < 0) & np.isfinite(best[mine])]
            chosen.append(c[np.argsort(-best[c], kind="stable")[:K]])
        fresh = np.concatenate(chosen)
        parent[fresh] = near[at[fresh], fresh]
        pad = np.full(4 + -fresh.size % 4, -1)
        v = decode(pick(now, np.concatenate([fresh, pad, parent[fresh], pad])))
        h = v.shape[1] // 2
        new = mx_ref.quantize(np.ascontiguousarray(((v[:, :h] + v[:, h:]) * np.float32(0.5)).astype(BF)))
        now = put(now, fresh, pick(new, np.arange(fresh.size)))
    y, pa = np.zeros((N, 128, O * P), np.float32), np.zeros((N, 1, P), np.float32)
    oc, osc = np.zeros((N, 128, 4 * P), np.uint8), np.zeros((N, 16, P), np.uint8)
    for r in range(N):
        mine = np.arange(P * r, P * r + P)
        q = pick(now, mine)
        for o in range(O): y[r, :, P * o:P * o + P] = mx_ref.matmul(mx_ref.quantize(np.ascontiguousarray(cut(w[r], o))), q)
        oc[r], osc[r] = emit(q)
        pa[r, 0] = parent[mine]
    return {"y": y, "oc": oc, "osc": osc, "pa": pa}

@@ -1,0 +1,499 @@
+from concourse.bass import DstId, RemoteDMATransfer
+from concourse.mybir import dt, AluOpType, AxisListType, ActivationFunctionType
+
+P, K, R, M, O = 128, 16, 3, 4, 3
+SEG = M + 1
+KEYW = SEG * (P + 1)
+BIG = 1.0e29
+TINY = 1.0e-37
+UNIT = 2.0 ** -12
+F32, BF16, F16, I32, U16, U8, CODE = "float32", "bfloat16", "float16", "int32", "uint16", "uint8", "float8_e4m3fn_x4"
+
+
+def _sb(n, d):
+    return ("sbuf", [128, n], d)
+
+
+SCRATCH = {
+    "xt": _sb(4 * P, BF16), "wt": _sb(512 * O, BF16), "et": _sb(2048, BF16), "ht": _sb(512, BF16),
+    "qa": _sb(512, CODE), "sa": _sb(512, U8), "qw": _sb(P * O, CODE), "sw": _sb(P * O, U8),
+    "qe": _sb(512, CODE), "se": _sb(512, U8), "qs": _sb(64, CODE), "ss": _sb(64, U8),
+    "qf": _sb(P, CODE), "sf": _sb(P, U8),
+    "sdi": _sb(4, I32), "nbi": _sb(32, I32), "nbf": _sb(4, F32), "osd": _sb(4, U16), "oid": _sb(2, U16), "omap": _sb(8, U16),
+    "pcol": _sb(1, F32), "row": _sb(P, F32), "idtab": _sb(2 * P, F32), "cj0": _sb(32, F32), "z32": _sb(32, F32),
+    "th": _sb(P, F32), "ones": _sb(P + 64, BF16), "rst": _sb(SEG * P, BF16), "rst16": _sb(P, F32), "e5": _sb(SEG * P, F16),
+    "am": _sb(P, BF16), "pen": _sb(P + 2, BF16), "kp": _sb(P + 2, F16), "x1": _sb(32, F32), "x2": _sb(32, F32), "thr": _sb(1, F32),
+    "r1": _sb(P, F32), "r2": _sb(P, F32), "dd": _sb(P, F32), "cc": _sb(P + 64, F32), "u1": _sb(P + 64, F32), "bs": _sb(P + 32, F32),
+    "sm": _sb(16, F32), "go": _sb(64, BF16), "dec": _sb(2048, BF16),
+    "srow": _sb(K, F32), "lif": _sb(P * R, F32), "pr": _sb(K, F32), "pw": _sb(2 * P, F32),
+    "dm": _sb(2 * P, F32), "mp": _sb(2 * P, F32), "mps": _sb(P, F32), "vr": _sb(K, F32), "val": _sb(K, F32),
+    "yw": _sb(2 * P * O, F32), "yn": _sb(K * O, F32),
+    "zb": ("psum", [128, 512], F32), "db": ("psum", [128, 2048], F32), "yb": ("psum", [128, 512 * O], F32),
+}
+for _t in range(R):
+    SCRATCH["lq%d" % _t] = _sb(P, CODE)
+    SCRATCH["ls%d" % _t] = _sb(P, U8)
+    SCRATCH["li%d" % _t] = _sb(P, U16)
+    SCRATCH["si%d" % _t] = _sb(K, U16)
+    SCRATCH["rq%d" % _t] = _sb(K, CODE)
+    SCRATCH["rs%d" % _t] = _sb(4 * K, U8)
+    SCRATCH["ri%d" % _t] = _sb(K, U16)
+    SCRATCH["of%d" % _t] = _sb(4, U16)
+    SCRATCH["zm%d" % _t] = _sb(P + 32, F32)
+for _t in range(R + 1):
+    SCRATCH["ky%d" % _t] = _sb(KEYW + 3, F16)
+
+SEMAPHORES = ["c_v", "c_s", "c_t", "c_g", "d_x", "d_sd", "d_nb", "d_w", "d_out", "gone"] + \
+    ["ai%d" % t for t in range(R)] + ["ac%d" % t for t in range(R)]
+
+A = AluOpType
+COPY = ActivationFunctionType.Copy
+SIGN = ActivationFunctionType.Sign
+SAME = ActivationFunctionType.Identity
+
+
+def V(name, c0, c1, step=1, p0=0, p1=128):
+    return (name, c0, c1, step, p0, p1)
+
+
+def _meet(a, b, other_queue):
+    if a[0] != b[0]:
+        return False
+    if SCRATCH[a[0]][0] == "psum" and other_queue:
+        return a[1] // 512 <= (b[2] - 1) // 512 and b[1] // 512 <= (a[2] - 1) // 512
+    if a[4] >= b[5] or b[4] >= a[5] or a[1] >= b[2] or b[1] >= a[2]:
+        return False
+    if a[3] == b[3] and a[3] > 1 and (a[1] - b[1]) % a[3]:
+        return False
+    return True
+
+
+def _mask(engines):
+    m = 0
+    for e in engines:
+        m |= 1 << e
+    return m
+
+
+def _dst(topo, dst, src):
+    rid, pid = topo.addr(dst, src)
+    return DstId(rid=rid, pnc=pid)
+
+
+def _common(topo, src, cores):
+    es = topo.engines(src, cores[0])
+    return [e for e in es if all(e in topo.engines(src, c) for c in cores)]
+
+
+def _routes(T, topo, rank):
+    me = T.cores[rank]
+    near = [q for q, c in enumerate(T.cores) if q != rank and topo.may_write(me, c)]
+    far = [q for q, c in enumerate(T.cores) if q != rank and not topo.may_write(me, c)]
+    free = sorted([c for c in topo.cores_of(me) if c not in T.cores], key=lambda c: (topo.die(c) != topo.die(me), c))
+    able = [c for c in free if all(topo.may_write(c, T.cores[q]) for q in far)]
+    plain = [c for c in free if c not in able]
+    return [(able[i], i, far) for i in range(3)] + [(plain[i], i, near) for i in range(3)]
+
+
+def _share(topo, me, helpers, pieces):
+    mine = [h for h in helpers if h[1] in pieces]
+    es = _common(topo, me, [h[0] for h in mine])
+    n = len(es) // len(mine)
+    return {h[0]: es[n * i:n * i + n] for i, h in enumerate(mine)}
+
+
+def relay_program(g, core, T, topo, rank, helpers, piece, dests):
+    n_in = len(_share(topo, T.cores[rank], helpers, (2,) if piece == 2 else (0, 1))[core])
+    cores = [T.cores[q] for q in dests]
+    es = _common(topo, core, cores)
+    a, b = K * rank, K * rank + K
+    for t in range(R):
+        if piece == 2:
+            sem, src, dst = "ai%d" % t, T["ri%d" % t][:, 0:K], T["li%d" % t][:, a:b]
+        elif piece == 0:
+            sem, src, dst = "ac%d" % t, T["rq%d" % t][:, 0:K].bitcast(dt.uint8), T["lq%d" % t][:, a:b].bitcast(dt.uint8)
+        else:
+            sem, src, dst = "ac%d" % t, T["rs%d" % t][:, 0:K], T["ls%d" % t][:, a:b]
+        g.wait_ge(T.sem[sem], n_in)
+        g.remote_dma_fused([RemoteDMATransfer(dst_ids=[_dst(topo, c, core) for c in cores], dma_engine_mask=_mask(es),
+                                              remote_sem=T.sem[sem], srcs=[src], dsts=[dst for c in cores])],
+                           local_sem=T.sem.gone)
+    g.wait_ge(T.sem.gone, R * len(es))
+
+
+def rank_program(g, core, T, topo):
+    rank = T.rank_of(core)
+    N = len(T.cores)
+    if rank is None:
+        for r in range(N):
+            helpers = _routes(T, topo, r)
+            for c, piece, dests in helpers:
+                if c == core:
+                    relay_program(g, core, T, topo, r, helpers, piece, dests)
+        return
+    helpers = _routes(T, topo, rank)
+    eng = {"v": g.vector, "s": g.scalar, "t": g.tensor, "g": g, "y": g.sync}
+    ops = []
+    hist = []
+    clock = {q: {} for q in eng}
+    known = {}
+    count = {q: 0 for q in eng}
+    total = {}
+    waited = set()
+
+    def ap(v):
+        if v[3] == 1:
+            return T[v[0]][v[4]:v[5], v[1]:v[2]]
+        return T[v[0]][v[4]:v[5], v[1]:v[2]:v[3]]
+
+    def issue(q, call, outs, ins, sem=None, track=True):
+        need = []
+        for view, wr, q2, tok in hist:
+            psum = SCRATCH[view[0]][0] == "psum" and q2 != q
+            hit = any(_meet(view, o, q2 != q) for o in outs) or ((wr or psum) and any(_meet(view, i, q2 != q) for i in ins))
+            if hit and tok not in need and (sem is None or tok[0] != sem):
+                need.append(tok)
+        need.sort(key=lambda k: -k[1])
+        waits = []
+        for tok in need:
+            if any(tok != o and known[o].get(tok[0], 0) >= tok[1] for o in need):
+                continue
+            if clock[q].get(tok[0], 0) < tok[1]:
+                waits.append(tok)
+                waited.add(tok)
+                for k, n in known[tok].items():
+                    clock[q][k] = max(clock[q].get(k, 0), n)
+        if sem is None:
+            count[q] += 1
+            tok = (q, count[q])
+        else:
+            tok = (sem, 1)
+            total[sem] = total.get(sem, 0) + 16
+        if track:
+            k = dict(clock[q])
+            if tok in known:
+                k = {a: min(n, known[tok].get(a, 0)) for a, n in k.items()}
+            k[tok[0]] = tok[1]
+            known[tok] = k
+            for o in outs:
+                hist.append((o, True, q, tok))
+            for i in ins:
+                hist.append((i, False, q, tok))
+        ops.append((q, call, waits, tok if track else None, sem))
+
+    def arrival(sem, n, outs):
+        total[sem] = n
+        known[(sem, 1)] = {sem: 1}
+        for o in outs:
+            hist.append((o, True, "far", (sem, 1)))
+
+    def views(*xs):
+        return [x for x in xs if isinstance(x, tuple)]
+
+    def arg(x):
+        return ap(x) if isinstance(x, tuple) else x
+
+    def ts(out, in0, s1, op0, s2=None, op1=None):
+        if op1 is None:
+            issue("v", lambda e: e.tensor_scalar(ap(out), ap(in0), arg(s1), None, op0), [out], views(in0, s1))
+        else:
+            issue("v", lambda e: e.tensor_scalar(ap(out), ap(in0), arg(s1), arg(s2), op0, op1), [out], views(in0, s1, s2))
+
+    def tt(out, in0, in1, op, off=None):
+        if off is None:
+            issue("v", lambda e: e.tensor_tensor(ap(out), ap(in0), ap(in1), op), [out], [in0, in1])
+        else:
+            issue("v", lambda e: e.tensor_tensor(ap(out), ap(in0).indirect(ap(off)), ap(in1), op), [out], [in0, in1, off])
+
+    def cp(q, out, in_, off=None):
+        ins = [in_] if off is None else [in_, off]
+        src = (lambda: ap(in_)) if off is None else (lambda: ap(in_).indirect(ap(off)))
+        if q == "v":
+            issue("v", lambda e: e.tensor_copy(ap(out), src()), [out], ins)
+        else:
+            issue("s", lambda e: e.activation(ap(out), src(), COPY), [out], ins)
+
+    def pick(qo, so, qi, si, off):
+        issue("v", lambda e: e.tensor_copy(ap(qo).bitcast(dt.uint32), ap(qi).bitcast(dt.uint32).indirect(ap(off))), [qo], [qi, off])
+        cp("s", so, si, off)
+
+    def act(out, in_, func, bias):
+        issue("s", lambda e: e.activation(ap(out), ap(in_), func, bias=ap(bias), scale=-1.0), [out], [in_, bias])
+
+    def scatter(win, vals, off):
+        issue("v", lambda e: e.tensor_copy(ap(win).indirect(ap(off)), ap(vals)), [win], [vals, off])
+
+    def red(out, in_, op, absolute=False):
+        if absolute:
+            issue("v", lambda e: e.tensor_reduce(ap(out), ap(in_), AxisListType.X, op, apply_absolute_value=True), [out], [in_])
+        else:
+            issue("v", lambda e: e.tensor_reduce(ap(out), ap(in_), AxisListType.X, op), [out], [in_])
+
+    def scan(out, d0, d1, init, op0=A.mult, op1=A.add):
+        issue("v", lambda e: e.tensor_tensor_scan(ap(out), ap(d0), ap(d1), arg(init), op0, op1), [out], views(d0, d1, init))
+
+    def fill(out, c):
+        issue("v", lambda e: e.memset(ap(out), c), [out], [])
+
+    def quant(q, s, in_):
+        issue("v", lambda e: e.quantize_mx(ap(q), ap(s), ap(in_)), [q, s], [in_])
+
+    def mm(out, wq, ws, xq, xs):
+        issue("t", lambda e: e.matmul_mx(ap(out), ap(wq), ap(ws), ap(xq), ap(xs), True, True), [out], [wq, ws, xq, xs])
+
+    def turn(out, in_):
+        issue("v", lambda e: e.transpose(ap(out), ap(in_)), [out], [in_])
+
+    def spread_a(r, x, c):
+        turn(V(r, 0, 32), V(x, c, c + 32))
+        turn(V(r, 32, 64, 1, 0, 64), V(x, c, c + 32, 1, 64, 128))
+        turn(V(r, 32, 64, 1, 64, 128), V(x, c, c + 32, 1, 0, 64))
+
+    def spread_b(r, queues):
+        for a in range(4):
+            b = a ^ 1
+            cp(queues[a], V(r, 64, 128, 1, 32 * a, 32 * a + 32), V(r, 0, 64, 1, 32 * b, 32 * b + 32))
+
+    def dma(q, sem, out, in_, outs, ins):
+        issue(q, lambda e: e.dma_start(out, in_), outs, ins, sem=sem)
+
+    sent = [0]
+    s0, s1 = K * rank, K * rank + K
+
+    def xfer(cores, es, sem, src, dst):
+        sent[0] += len(es)
+        return RemoteDMATransfer(dst_ids=[_dst(topo, c, core) for c in cores], dma_engine_mask=_mask(es),
+                                 remote_sem=T.sem[sem], srcs=[src], dsts=[dst for c in cores])
+
+    def fused(xs, ins):
+        issue("g", lambda e: e.remote_dma_fused(xs, local_sem=T.sem.gone), [], ins, track=False)
+
+    def post_ids(t):
+        src = V("si%d" % t, 0, K)
+        share = _share(topo, core, helpers, (2,))
+        fused([xfer([c], es, "ai%d" % t, ap(src), T["ri%d" % t][:, 0:K]) for c, es in share.items()], [src])
+
+    def post_cols(t, qn, sn, c0):
+        q, s4 = V(qn, c0, c0 + K), V(sn, c0, c0 + 4 * K)
+        share = _share(topo, core, helpers, (0, 1))
+        xs = []
+        for c, piece, dests in helpers:
+            if piece == 0:
+                xs.append(xfer([c], share[c], "ac%d" % t, ap(q).bitcast(dt.uint8), T["rq%d" % t][:, 0:K].bitcast(dt.uint8)))
+            elif piece == 1:
+                xs.append(xfer([c], share[c], "ac%d" % t, ap(s4), T["rs%d" % t][:, 0:4 * K]))
+        fused(xs, [q, s4])
+
+    n_arr = [0, 0, 0]
+    for q in range(N):
+        for c, piece, dests in _routes(T, topo, q):
+            if rank in dests:
+                n_arr[piece] += len(_common(topo, c, [T.cores[u] for u in dests]))
+    for t in range(R):
+        others = [(K * q, K * q + K) for q in range(N) if q != rank]
+        arrival("ai%d" % t, n_arr[2], [V("li%d" % t, a, b) for a, b in others])
+        arrival("ac%d" % t, n_arr[0] + n_arr[1], [V(n % t, a, b) for a, b in others for n in ("lq%d", "ls%d")])
+
+    pcol = V("pcol", 0, 1)
+    row = V("row", 0, P)
+    g0 = float(P * rank)
+
+    for h in range(2):
+        dma("s", "d_sd", T.sdi[16 * h:16 * h + 16, 0:1], T.sd[:], [V("sdi", 0, 1, 1, 16 * h, 16 * h + 16)], [])
+    dma("y", "d_x", T.xt[:], T.x[:], [V("xt", 0, 512)], [])
+    for h in range(8):
+        dma("y" if h % 2 else "s", "d_nb", T.nbi[16 * h:16 * h + 16, 0:25], T.nb[:, h:h + 25], [V("nbi", 0, 25, 1, 16 * h, 16 * h + 16)], [])
+    dma("y", "d_w", T.wt[:], T.w[:], [V("wt", 0, 512 * O)], [])
+
+    issue("g", lambda e: e.iota(ap(row), [[1, P]], 0, 0, allow_small_or_imprecise_dtypes=True), [row], [])
+    issue("g", lambda e: e.iota(ap(pcol), [[1, 1]], 0, 1, allow_small_or_imprecise_dtypes=True), [pcol], [])
+    issue("g", lambda e: e.iota(T.cj0[:, 0:32], [[0, 2], [-1, 16]], 0, 0, allow_small_or_imprecise_dtypes=True), [V("cj0", 0, 32)], [])
+    fill(V("osd", 0, 4), 0)
+    fill(V("idtab", P, 2 * P), 4000.0)
+    fill(V("et", 0, 2048), 0.0)
+    ts(V("idtab", 0, P), row, g0, A.add)
+    for a in range(4):
+        cp("v", V("osd", 0, 1, 1, 32 * a, 32 * a + 32), V("sdi", 0, 1, 1, 0, 32))
+    cp("v", V("si0", 0, K), V("idtab", 0, 2 * P), V("osd", 0, 1))
+    post_ids(0)
+    quant(V("qa", 0, P), V("sa", 0, P), V("xt", 0, 512))
+    pick(V("qs", 0, 64), V("ss", 0, 64), V("qa", 0, P), V("sa", 0, P), V("osd", 0, 4))
+    post_cols(0, "qs", "ss", 0)
+
+    for b in range(4):
+        ts(V("et", 512 * b + b, 512 * b + 512, 4), row, pcol, A.is_equal, 0.5, A.mult)
+    quant(V("qe", 0, 512), V("se", 0, 512), V("et", 0, 2048))
+
+    def decode(qn, sn, c):
+        for b in range(4):
+            mm(V("db", 512 * b, 512 * b + P), V("qe", P * b, P * b + P), V("se", P * b, P * b + P), V(qn, c, c + P), V(sn, c, c + P))
+
+    def keep(b, at):
+        cp("s", V("dec", 512 * b + at, 512 * b + at + P), V("db", 512 * b, 512 * b + P))
+
+    pick(V("lq0", s0, s1), V("ls0", s0, s1), V("qa", 0, P), V("sa", 0, P), V("osd", 0, 1))
+    decode("qa", "sa", 0)
+    for b in range(4):
+        keep(b, 0)
+    cp("v", V("li0", s0, s1), V("si0", 0, K))
+    cp("v", V("nbf", 0, 4), V("nbi", 0, 25, 8))
+    fill(V("rst", 0, SEG * P), 1.0)
+    fill(V("z32", 0, 32), 0.0)
+    fill(V("zm0", P, P + 32), -BIG)
+    ts(V("e5", 0, SEG * P, SEG), row, -704.0, A.add, UNIT, A.mult)
+    fill(V("rst", 0, SEG * P, SEG), 0.0)
+    ts(V("ky0", KEYW - 1, KEYW), V("z32", 0, 1), -704.0 * UNIT, A.add)
+    cp("v", V("srow", 0, K), V("idtab", 0, P), V("osd", 0, 1))
+    ts(V("x1", 0, 32), V("z32", 0, 32), pcol, A.add)
+    fill(V("pw", 0, 2 * P), -1.0)
+    ts(V("sm", 1, 2), pcol, g0, A.add)
+    spread_a("r1", "x1", 0)
+    ts(V("val", 0, K), V("srow", 0, K), V("sm", 1, 2), A.is_equal)
+    spread_b("r1", "vvvv")
+    red(V("sm", 0, 1), V("val", 0, K), A.max)
+    scatter(V("pw", 0, 2 * P), V("srow", 0, K), V("osd", 0, 1))
+    ts(V("th", 0, P), V("r1", 0, P), pcol, A.is_ge, -TINY, A.mult)
+    ts(V("thr", 0, 1), V("sm", 0, 1), 8.0, A.mult, -256.0 * UNIT, A.add)
+    ts(V("cc", 30, 31), pcol, 1024.0 / 2 ** 19, A.mult, 192.0 / 2 ** 19, A.add)
+    fill(V("ones", 0, P + 64), 1.0)
+    fill(V("cc", P + 32, P + 64), -1.0)
+    fill(V("ht", 0, 512), 0.0)
+    fill(V("cc", P + 32, P + 33), 0.0)
+    fill(V("cc", P + 32 + K, P + 33 + K), K - 1.0)
+    turn(V("x2", 0, 32), V("cj0", 0, 32))
+    ts(V("oid", 0, 1), V("x2", 0, 1), -1.0, A.mult)
+
+    def late_constants():
+        fill(V("rst16", 0, P), 1.0)
+        fill(V("dm", P, 2 * P), 0.0)
+        for a in range(4):
+            ts(V("dm", 32 * a, 32 * a + 32), V("cj0", 0, 32), V("x2", 0, 1), A.is_equal)
+        fill(V("rst16", 0, P, 16), 0.0)
+        tt(V("mp", 0, P), V("dm", 0, P), row, A.mult)
+
+    def products_w(c):
+        for o in range(O):
+            mm(V("yb", 512 * o, 512 * o + P), V("qw", P * o, P * o + P), V("sw", P * o, P * o + P), V("qa", c, c + P), V("sa", c, c + P))
+
+    def y_out(o):
+        cp("s", V("yn", K * o, K * o + K), V("yb", 512 * o, 512 * o + K))
+
+    def y_put(o, hi):
+        scatter(V("yw", 2 * P * o, 2 * P * o + 2 * P), V("yn", K * o, K * o + K), hi)
+
+    for t in range(R):
+        li, lq, ls = V("li%d" % t, 0, P), V("lq%d" % t, 0, P), V("ls%d" % t, 0, P)
+        ky, kn, zm, zn = "ky%d" % t, "ky%d" % (t + 1), "zm%d" % t, "zm%d" % (t + 1)
+        best, km, ib = V("bs", P, P + 1), V(kn, KEYW - 1, KEYW), V("cc", 31, 32)
+        hi, lo = V("of%d" % t, 0, 1), V("of%d" % t, 2, 3)
+        last = t + 1 == R
+        c = P * (t + 1)
+        for k in range(M):
+            ts(V("e5", 1 + k, SEG * P, SEG), li, V("nbf", k, k + 1), A.is_equal, 512.0 * (M - k) * UNIT, A.mult)
+        scan(V(ky, 0, SEG * P), V("rst", 0, SEG * P), V("e5", 0, SEG * P), 0.0)
+        ts(V("am", 0, P), V(ky, M, SEG * P, SEG), V("thr", 0, 1), A.is_lt, -BIG, A.mult)
+        if last:
+            cp("v", V("lif", P * t, P * t + P), li)
+        mm(V("zb", 0, P), V("qa", 0, P), V("sa", 0, P), lq, ls)
+        decode(lq[0], ls[0], 0)
+        tt(V(zm, 0, P), V("zb", 0, P), V("am", 0, P), A.add)
+        scan(V("bs", 0, P + 32), V(zm, 0, P + 32), V(zm, 0, P + 32), -2.0 * BIG, A.max, A.max)
+        act(V("pen", 0, P + 1), V(zm, 0, P + 1), SIGN, best)
+        spread_a("r1", "bs", P)
+        spread_b("r1", "ssss")
+        act(V("dd", 0, P), V("r1", 0, P), SAME, best)
+        for b in range(4):
+            keep(b, c)
+        tt(V("kp", 0, P + 1), V(ky, M, KEYW, SEG), V("pen", 0, P + 1), A.subtract)
+        ts(ib, best, -0.1 * BIG, A.is_lt, 0.25, A.mult)
+        scan(V(kn, KEYW - P - 1, KEYW), V("kp", 0, P + 1), V("kp", 0, P + 1), -2.0, A.max, A.max)
+        ts(V("sm", 3, 4), km, 1.5 * 2 ** 20, A.add, 1.5 * 2 ** 20, A.subtract)
+        tt(V("cc", 32, P + 32), V("dd", 0, P), V("th", 0, P), A.is_le)
+        ts(V("sm", 4, 5), km, V("sm", 3, 4), A.subtract, 2.0 ** -7, A.mult)
+        scan(V("u1", 30, P + 64), V("ones", 30, P + 64), V("cc", 30, P + 64), V("sm", 4, 5))
+        u1 = V("u1", P + 31, P + 32)
+        spread_a("r2", "u1", P + 32)
+        spread_b("r2", "vsvs")
+        red(V("sm", 5, 6), V("r2", 0, P), A.min, True)
+        ts(hi, V("sm", 5, 6), 512.0, A.mult)
+        ts(V("sm", 6, 7), V("sm", 5, 6), 1.5 * 2 ** 14, A.add, 1.5 * 2 ** 14, A.subtract)
+        if not last:
+            cp("v", V("si%d" % (t + 1), 0, K), V("idtab", 0, 2 * P), hi)
+            post_ids(t + 1)
+        else:
+            tt(V("val", 0, K), V("dm", 0, 2 * P), V("vr", 0, K), A.mult, hi)
+        ts(lo, V("sm", 5, 6), V("sm", 6, 7), A.subtract, 2.0 ** 19, A.mult)
+        for b in range(4):
+            cp("s", V("go", K * b, K * b + K), V("dec", 512 * b, 512 * b + 2 * P), hi)
+        for b in range(4):
+            tt(V("ht", b, 4 * K, 4), V("dec", 512 * b + P, 512 * b + P * (t + 2)), V("go", K * b, K * b + K), A.add, lo)
+        if last:
+            scatter(V("mp", 0, 2 * P), V("val", 0, K), hi)
+        quant(V("qa", c, c + P), V("sa", c, c + P), V("ht", 0, 512))
+        if not last:
+            post_cols(t + 1, "qa", "sa", c)
+            pick(V("lq%d" % (t + 1), s0, s1), V("ls%d" % (t + 1), s0, s1), V("qa", c, c + P), V("sa", c, c + P), V("oid", 0, 1))
+            cp("v", V("li%d" % (t + 1), s0, s1), V("si%d" % (t + 1), 0, K))
+            ts(V("e5", 0, SEG * P, SEG), row, float(c) - 704.0, A.add, UNIT, A.mult)
+            ts(V("sm", 7, 8), ib, 100.0, A.mult, u1, A.add)
+            fill(V(zn, P + 1, P + 32), -BIG)
+            ts(V("sm", 8, 9), V("sm", 7, 8), float(K), A.is_lt, 8.0, A.mult)
+            tt(V("thr", 0, 1), V("thr", 0, 1), V("sm", 8, 9), A.add)
+            ts(V("sm", 9, 10), V("thr", 0, 1), 1.0, A.is_lt, 2.0 * BIG, A.mult)
+            ts(V(zn, P, P + 1), V("sm", 9, 10), -BIG, A.add, best, A.min)
+            if t == 0:
+                quant(V("qw", 0, P * O), V("sw", 0, P * O), V("wt", 0, 512 * O))
+                late_constants()
+                products_w(0)
+                for o in range(O):
+                    cp("s", V("yw", 2 * P * o, 2 * P * o + P), V("yb", 512 * o, 512 * o + P))
+                ts(V("vr", 0, K), V("row", 0, K), float(c), A.add)
+            cp("v", V("lif", P * t, P * t + P), li)
+        products_w(c)
+        cp("s", V("pr", 0, K), V("lif", 0, c), lo)
+        if not last:
+            tt(V("val", 0, K), V("dm", 0, 2 * P), V("vr", 0, K), A.mult, hi)
+            scatter(V("mp", 0, 2 * P), V("val", 0, K), hi)
+            for o in range(O):
+                y_out(o)
+                y_put(o, hi)
+            scatter(V("pw", 0, 2 * P), V("pr", 0, K), hi)
+            ts(V("vr", 0, K), V("row", 0, K), float(c + P), A.add)
+        else:
+            scan(V("mps", 0, P), V("rst16", 0, P), V("mp", 0, P), 0.0)
+            scatter(V("pw", 0, 2 * P), V("pr", 0, K), hi)
+            dma("y", "d_out", T.pa[:], T.pw[0:1, 0:P], [], [V("pw", 0, P)])
+            cp("v", V("omap", 0, 8), V("mps", 15, P, 16))
+            y_out(0)
+            pick(V("qf", 0, P), V("sf", 0, P), V("qa", 0, 512), V("sa", 0, 512), V("omap", 0, 8))
+            y_out(1)
+            y_out(2)
+            dma("y", "d_out", T.oc[:], T.qf[:, 0:P].bitcast(dt.uint8), [], [V("qf", 0, P)])
+            y_put(0, hi)
+            dma("y", "d_out", T.y[:, 0:P], T.yw[:, 0:P], [], [V("yw", 0, P)])
+            y_put(1, hi)
+            dma("y", "d_out", T.y[:, P:2 * P], T.yw[:, 2 * P:3 * P], [], [V("yw", 2 * P, 3 * P)])
+            for a in range(4):
+                dma("s", "d_out", T.osc[4 * a:4 * a + 4, 0:P], T.sf[32 * a:32 * a + 4, 0:P], [], [V("sf", 0, P)])
+            y_put(2, hi)
+            dma("y", "d_out", T.y[:, 2 * P:3 * P], T.yw[:, 4 * P:5 * P], [], [V("yw", 4 * P, 5 * P)])
+
+    value = {}
+    run = {q: 0 for q in eng}
+    for q, call, waits, tok, sem in ops:
+        if sem is None and tok in waited:
+            run[q] += 1
+            value[tok] = run[q]
+    for q, call, waits, tok, sem in ops:
+        for w in waits:
+            if w in value:
+                eng[q].wait_ge(T.sem["c_" + w[0]], value[w])
+            else:
+                eng[q].wait_ge(T.sem[w[0]], total[w[0]])
+        ins = call(eng[q])
+        if sem is not None:
+            ins.then_inc(T.sem[sem], 16)
+        elif tok in value:
+            ins.then_inc(T.sem["c_" + q], 1)
+    g.wait_ge(T.sem.gone, sent[0])
+    g.sync.wait_ge(T.sem.d_out, total["d_out"])

@@ -4,9 +4,10 @@ from concourse.mybir import dt, AluOpType, AxisListType, ActivationFunctionType
 P, K, R, M, O = 128, 16, 3, 4, 3
 SEG = M + 1
 KEYW = SEG * (P + 1)
-BIG = 1.0e29
+BIG = 2.0 ** 96
 TINY = 1.0e-37
-UNIT = 2.0 ** -12
+UNIT = 2.0 ** -20
+BLOCK = (0, 2, 1, 3)
 F32, BF16, F16, I32, U16, U8, CODE = "float32", "bfloat16", "float16", "int32", "uint16", "uint8", "float8_e4m3fn_x4"
 
 
@@ -15,19 +16,21 @@ def _sb(n, d):
 
 
 SCRATCH = {
-    "xt": _sb(4 * P, BF16), "wt": _sb(512 * O, BF16), "et": _sb(2048, BF16), "ht": _sb(512, BF16),
+    "xt": _sb(4 * P, BF16), "wt": _sb(512 * O, BF16), "et": _sb(2048, BF16), "ht": _sb(512, BF16), "zt": _sb(512, BF16),
     "qa": _sb(512, CODE), "sa": _sb(512, U8), "qw": _sb(P * O, CODE), "sw": _sb(P * O, U8),
-    "qe": _sb(512, CODE), "se": _sb(512, U8), "qs": _sb(64, CODE), "ss": _sb(64, U8),
-    "qf": _sb(P, CODE), "sf": _sb(P, U8),
+    "qe": _sb(512, CODE), "se": _sb(512, U8), "qs": _sb(P + K, CODE), "ss": _sb(P + K, U8),
+    "qf": _sb(P, CODE), "sf": _sb(P, U8), "qp": _sb(P, CODE), "sp": _sb(P, U8),
     "sdi": _sb(4, I32), "nbi": _sb(32, I32), "nbf": _sb(4, F32), "osd": _sb(4, U16), "oid": _sb(2, U16), "omap": _sb(8, U16),
+    "opm": _sb(8, U16), "c8": _sb(8, F32), "plc": _sb(1, F32),
     "pcol": _sb(1, F32), "row": _sb(P, F32), "idtab": _sb(2 * P, F32), "cj0": _sb(32, F32), "z32": _sb(32, F32),
-    "th": _sb(P, F32), "ones": _sb(P + 64, BF16), "rst": _sb(SEG * P, BF16), "rst16": _sb(P, F32), "e5": _sb(SEG * P, F16),
+    "th": _sb(32, F32), "tl": _sb(2, F32), "rst": _sb(SEG * P, BF16), "rst16": _sb(P, F32), "e5": _sb(SEG * P, F16),
     "am": _sb(P, BF16), "pen": _sb(P + 2, BF16), "kp": _sb(P + 2, F16), "x1": _sb(32, F32), "x2": _sb(32, F32), "thr": _sb(1, F32),
-    "r1": _sb(P, F32), "r2": _sb(P, F32), "dd": _sb(P, F32), "cc": _sb(P + 64, F32), "u1": _sb(P + 64, F32), "bs": _sb(P + 32, F32),
+    "r1": _sb(64, F32), "r2": _sb(P, F32), "dd": _sb(96, F32), "ca": _sb(98, BF16), "cb": _sb(162, F16), "u1": _sb(97, F32),
+    "bs": _sb(96, F32), "pc": _sb(2, F32), "c4": _sb(8, F32),
     "sm": _sb(16, F32), "go": _sb(64, BF16), "dec": _sb(2048, BF16),
-    "srow": _sb(K, F32), "lif": _sb(P * R, F32), "pr": _sb(K, F32), "pw": _sb(2 * P, F32),
+    "srow": _sb(K, F32), "lif": _sb(P * R, F32),
     "dm": _sb(2 * P, F32), "mp": _sb(2 * P, F32), "mps": _sb(P, F32), "vr": _sb(K, F32), "val": _sb(K, F32),
-    "yw": _sb(2 * P * O, F32), "yn": _sb(K * O, F32),
+    "yw": _sb(2 * P * (O + 1), F32),
     "zb": ("psum", [128, 512], F32), "db": ("psum", [128, 2048], F32), "yb": ("psum", [128, 512 * O], F32),
 }
 for _t in range(R):
@@ -38,10 +41,10 @@ for _t in range(R):
     SCRATCH["rq%d" % _t] = _sb(K, CODE)
     SCRATCH["rs%d" % _t] = _sb(4 * K, U8)
     SCRATCH["ri%d" % _t] = _sb(K, U16)
-    SCRATCH["of%d" % _t] = _sb(4, U16)
+    SCRATCH["of%d" % _t] = _sb(6, U16)
     SCRATCH["zm%d" % _t] = _sb(P + 32, F32)
-for _t in range(R + 1):
     SCRATCH["ky%d" % _t] = _sb(KEYW + 3, F16)
+    SCRATCH["yn%d" % _t] = _sb(K * (O + 1), F32)
 
 SEMAPHORES = ["c_v", "c_s", "c_t", "c_g", "d_x", "d_sd", "d_nb", "d_w", "d_out", "gone"] + \
     ["ai%d" % t for t in range(R)] + ["ac%d" % t for t in range(R)]
@@ -50,6 +53,8 @@ A = AluOpType
 COPY = ActivationFunctionType.Copy
 SIGN = ActivationFunctionType.Sign
 SAME = ActivationFunctionType.Identity
+RELU = ActivationFunctionType.Relu
+CODES, SCALES, IDS = 0, 1, 2
 
 
 def V(name, c0, c1, step=1, p0=0, p1=128):
@@ -87,38 +92,50 @@ def _common(topo, src, cores):
 
 def _routes(T, topo, rank):
     me = T.cores[rank]
-    near = [q for q, c in enumerate(T.cores) if q != rank and topo.may_write(me, c)]
-    far = [q for q, c in enumerate(T.cores) if q != rank and not topo.may_write(me, c)]
+    n = len(T.cores)
+    ring = [(rank + i) % n for i in range(1, n)]
+    near = [q for q in ring if topo.may_write(me, T.cores[q])]
+    far = [q for q in ring if q not in near]
     free = sorted([c for c in topo.cores_of(me) if c not in T.cores], key=lambda c: (topo.die(c) != topo.die(me), c))
     able = [c for c in free if all(topo.may_write(c, T.cores[q]) for q in far)]
-    plain = [c for c in free if c not in able]
-    return [(able[i], i, far) for i in range(3)] + [(plain[i], i, near) for i in range(3)]
+    out = _common(topo, me, [T.cores[q] for q in near])
+    every = _common(topo, me, free)
+    home = [e for e in every if e not in out]
+    e4 = [every[4 * i:4 * i + 4] for i in range(4)]
+    straight = [(T.cores[q], None) for q in near]
+    ids = [[(IDS, home[:4], [(able[1], far[:2])]), (IDS, home[4:], [(able[3], far[2:])]), (IDS, out, straight)]]
+    cols = [[(CODES, e4[2], [(able[0], far[:2])]), (CODES, e4[3], [(able[2], far[2:])]),
+             (SCALES, e4[0], [(able[1], far[:2])]), (SCALES, e4[1], [(able[3], far[2:])])],
+            [(CODES, out, straight)], [(SCALES, out, straight)]]
+    return ids, cols
 
 
-def _share(topo, me, helpers, pieces):
-    mine = [h for h in helpers if h[1] in pieces]
-    es = _common(topo, me, [h[0] for h in mine])
-    n = len(es) // len(mine)
-    return {h[0]: es[n * i:n * i + n] for i, h in enumerate(mine)}
-
-
-def relay_program(g, core, T, topo, rank, helpers, piece, dests):
-    n_in = len(_share(topo, T.cores[rank], helpers, (2,) if piece == 2 else (0, 1))[core])
-    cores = [T.cores[q] for q in dests]
-    es = _common(topo, core, cores)
+def relay_program(g, core, T, topo, rank, routes):
     a, b = K * rank, K * rank + K
+    gone = 0
     for t in range(R):
-        if piece == 2:
-            sem, src, dst = "ai%d" % t, T["ri%d" % t][:, 0:K], T["li%d" % t][:, a:b]
-        elif piece == 0:
-            sem, src, dst = "ac%d" % t, T["rq%d" % t][:, 0:K].bitcast(dt.uint8), T["lq%d" % t][:, a:b].bitcast(dt.uint8)
-        else:
-            sem, src, dst = "ac%d" % t, T["rs%d" % t][:, 0:K], T["ls%d" % t][:, a:b]
-        g.wait_ge(T.sem[sem], n_in)
-        g.remote_dma_fused([RemoteDMATransfer(dst_ids=[_dst(topo, c, core) for c in cores], dma_engine_mask=_mask(es),
-                                              remote_sem=T.sem[sem], srcs=[src], dsts=[dst for c in cores])],
-                           local_sem=T.sem.gone)
-    g.wait_ge(T.sem.gone, R * len(es))
+        for calls in routes:
+            for call in calls:
+                for piece, given, targets in call:
+                    for c, dests in targets:
+                        if c != core:
+                            continue
+                        cores = [T.cores[q] for q in dests]
+                        es = _common(topo, core, cores)
+                        if piece == IDS:
+                            sem, src, dst = "ai%d" % t, T["ri%d" % t][:, 0:K], T["li%d" % t][:, a:b]
+                        elif piece == CODES:
+                            sem = "ac%d" % t
+                            src, dst = T["rq%d" % t][:, 0:K].bitcast(dt.uint8), T["lq%d" % t][:, a:b].bitcast(dt.uint8)
+                        else:
+                            sem, src, dst = "ac%d" % t, T["rs%d" % t][:, 0:K], T["ls%d" % t][:, a:b]
+                        g.wait_ge(T.sem[sem], len(given))
+                        g.remote_dma_fused([RemoteDMATransfer(dst_ids=[_dst(topo, u, core) for u in cores],
+                                                              dma_engine_mask=_mask(es), remote_sem=T.sem[sem], srcs=[src],
+                                                              dsts=[dst for u in cores])], local_sem=T.sem.gone)
+                        gone += len(es)
+    if gone:
+        g.wait_ge(T.sem.gone, gone)
 
 
 def rank_program(g, core, T, topo):
@@ -126,12 +143,9 @@ def rank_program(g, core, T, topo):
     N = len(T.cores)
     if rank is None:
         for r in range(N):
-            helpers = _routes(T, topo, r)
-            for c, piece, dests in helpers:
-                if c == core:
-                    relay_program(g, core, T, topo, r, helpers, piece, dests)
+            relay_program(g, core, T, topo, r, _routes(T, topo, r))
         return
-    helpers = _routes(T, topo, rank)
+    routes = _routes(T, topo, rank)
     eng = {"v": g.vector, "s": g.scalar, "t": g.tensor, "g": g, "y": g.sync}
     ops = []
     hist = []
@@ -193,6 +207,9 @@ def rank_program(g, core, T, topo):
     def arg(x):
         return ap(x) if isinstance(x, tuple) else x
 
+    def part(v, p0, p1):
+        return v[:4] + (p0, p1)
+
     def ts(out, in0, s1, op0, s2=None, op1=None):
         if op1 is None:
             issue("v", lambda e: e.tensor_scalar(ap(out), ap(in0), arg(s1), None, op0), [out], views(in0, s1))
@@ -244,84 +261,106 @@ def rank_program(g, core, T, topo):
     def turn(out, in_):
         issue("v", lambda e: e.transpose(ap(out), ap(in_)), [out], [in_])
 
-    def spread_a(r, x, c):
-        turn(V(r, 0, 32), V(x, c, c + 32))
-        turn(V(r, 32, 64, 1, 0, 64), V(x, c, c + 32, 1, 64, 128))
-        turn(V(r, 32, 64, 1, 64, 128), V(x, c, c + 32, 1, 0, 64))
-
-    def spread_b(r, queues):
-        for a in range(4):
-            b = a ^ 1
-            cp(queues[a], V(r, 64, 128, 1, 32 * a, 32 * a + 32), V(r, 0, 64, 1, 32 * b, 32 * b + 32))
-
     def dma(q, sem, out, in_, outs, ins):
         issue(q, lambda e: e.dma_start(out, in_), outs, ins, sem=sem)
+
+    def iota(out, pattern, mult):
+        issue("g", lambda e: e.iota(ap(out), pattern, 0, mult, allow_small_or_imprecise_dtypes=True), [out], [])
 
     sent = [0]
     s0, s1 = K * rank, K * rank + K
 
-    def xfer(cores, es, sem, src, dst):
-        sent[0] += len(es)
-        return RemoteDMATransfer(dst_ids=[_dst(topo, c, core) for c in cores], dma_engine_mask=_mask(es),
-                                 remote_sem=T.sem[sem], srcs=[src], dsts=[dst for c in cores])
-
-    def fused(xs, ins):
-        issue("g", lambda e: e.remote_dma_fused(xs, local_sem=T.sem.gone), [], ins, track=False)
+    def post(calls, t, qn, sn, c0):
+        for call in calls:
+            wide = any(piece == CODES for piece, es, targets in call)
+            xs, ins = [], []
+            for piece, es, targets in call:
+                if piece == IDS:
+                    v, sem = V("si%d" % t, 0, K), "ai%d" % t
+                    src, mid, end = ap(v), T["ri%d" % t][:, 0:K], T["li%d" % t][:, s0:s1]
+                elif piece == CODES:
+                    v, sem = V(qn, c0, c0 + K), "ac%d" % t
+                    src = ap(v).bitcast(dt.uint8)
+                    mid, end = T["rq%d" % t][:, 0:K].bitcast(dt.uint8), T["lq%d" % t][:, s0:s1].bitcast(dt.uint8)
+                else:
+                    n = 4 * K if wide else K
+                    v, sem = V(sn, c0, c0 + n), "ac%d" % t
+                    src, mid, end = ap(v), T["rs%d" % t][:, 0:n], T["ls%d" % t][:, s0:s1]
+                sent[0] += len(es)
+                ins.append(v)
+                xs.append(RemoteDMATransfer(dst_ids=[_dst(topo, c, core) for c, d in targets], dma_engine_mask=_mask(es),
+                                            remote_sem=T.sem[sem], srcs=[src],
+                                            dsts=[end if d is None else mid for c, d in targets]))
+            issue("g", lambda e, xs=xs: e.remote_dma_fused(xs, local_sem=T.sem.gone), [], ins, track=False)
 
     def post_ids(t):
-        src = V("si%d" % t, 0, K)
-        share = _share(topo, core, helpers, (2,))
-        fused([xfer([c], es, "ai%d" % t, ap(src), T["ri%d" % t][:, 0:K]) for c, es in share.items()], [src])
+        post(routes[0], t, None, None, 0)
 
     def post_cols(t, qn, sn, c0):
-        q, s4 = V(qn, c0, c0 + K), V(sn, c0, c0 + 4 * K)
-        share = _share(topo, core, helpers, (0, 1))
-        xs = []
-        for c, piece, dests in helpers:
-            if piece == 0:
-                xs.append(xfer([c], share[c], "ac%d" % t, ap(q).bitcast(dt.uint8), T["rq%d" % t][:, 0:K].bitcast(dt.uint8)))
-            elif piece == 1:
-                xs.append(xfer([c], share[c], "ac%d" % t, ap(s4), T["rs%d" % t][:, 0:4 * K]))
-        fused(xs, [q, s4])
+        post(routes[1], t, qn, sn, c0)
 
     n_arr = [0, 0, 0]
     for q in range(N):
-        for c, piece, dests in _routes(T, topo, q):
-            if rank in dests:
-                n_arr[piece] += len(_common(topo, c, [T.cores[u] for u in dests]))
+        for calls in _routes(T, topo, q):
+            for call in calls:
+                for piece, es, targets in call:
+                    for c, dests in targets:
+                        if dests is None:
+                            n_arr[piece] += len(es) if c == core else 0
+                        elif rank in dests:
+                            n_arr[piece] += len(_common(topo, c, [T.cores[u] for u in dests]))
+    others = [(K * q, K * q + K) for q in range(N) if q != rank]
     for t in range(R):
-        others = [(K * q, K * q + K) for q in range(N) if q != rank]
-        arrival("ai%d" % t, n_arr[2], [V("li%d" % t, a, b) for a, b in others])
-        arrival("ac%d" % t, n_arr[0] + n_arr[1], [V(n % t, a, b) for a, b in others for n in ("lq%d", "ls%d")])
+        arrival("ai%d" % t, n_arr[IDS], [V("li%d" % t, a, b) for a, b in others])
+        arrival("ac%d" % t, n_arr[CODES] + n_arr[SCALES], [V(n % t, a, b) for a, b in others for n in ("lq%d", "ls%d")])
 
-    pcol = V("pcol", 0, 1)
+    pcol, plc = V("pcol", 0, 1), V("plc", 0, 1)
     row = V("row", 0, P)
     g0 = float(P * rank)
+    pw = 2 * P * O
 
     for h in range(2):
         dma("s", "d_sd", T.sdi[16 * h:16 * h + 16, 0:1], T.sd[:], [V("sdi", 0, 1, 1, 16 * h, 16 * h + 16)], [])
     dma("y", "d_x", T.xt[:], T.x[:], [V("xt", 0, 512)], [])
     for h in range(8):
-        dma("y" if h % 2 else "s", "d_nb", T.nbi[16 * h:16 * h + 16, 0:25], T.nb[:, h:h + 25], [V("nbi", 0, 25, 1, 16 * h, 16 * h + 16)], [])
-    dma("y", "d_w", T.wt[:], T.w[:], [V("wt", 0, 512 * O)], [])
+        u = 2 * BLOCK[h // 2] + h % 2
+        dma("y", "d_nb", T.nbi[16 * h:16 * h + 16, 0:25], T.nb[:, u:u + 25], [V("nbi", 0, 25, 1, 16 * h, 16 * h + 16)], [])
+    dma("y", "d_w", T.wt[:], T.w[:], [V("wt", 0, 512 * O)], [V("li0", others[0][0], others[0][1])])
 
-    issue("g", lambda e: e.iota(ap(row), [[1, P]], 0, 0, allow_small_or_imprecise_dtypes=True), [row], [])
-    issue("g", lambda e: e.iota(ap(pcol), [[1, 1]], 0, 1, allow_small_or_imprecise_dtypes=True), [pcol], [])
-    issue("g", lambda e: e.iota(T.cj0[:, 0:32], [[0, 2], [-1, 16]], 0, 0, allow_small_or_imprecise_dtypes=True), [V("cj0", 0, 32)], [])
-    fill(V("osd", 0, 4), 0)
+    iota(row, [[1, P]], 0)
+    iota(pcol, [[1, 1]], 1)
+    iota(V("cj0", 0, 32), [[0, 2], [-1, 16]], 0)
+    iota(V("c8", 0, 8), [[32 * BLOCK[2], 2], [32 * BLOCK[1], 2], [16, 2]], 0)
+    fill(V("zt", 0, 512), 0.0)
     fill(V("idtab", P, 2 * P), 4000.0)
-    fill(V("et", 0, 2048), 0.0)
+    quant(V("qs", K, K + P), V("ss", K, K + P), V("zt", 0, 512))
     ts(V("idtab", 0, P), row, g0, A.add)
     for a in range(4):
         cp("v", V("osd", 0, 1, 1, 32 * a, 32 * a + 32), V("sdi", 0, 1, 1, 0, 32))
     cp("v", V("si0", 0, K), V("idtab", 0, 2 * P), V("osd", 0, 1))
     post_ids(0)
     quant(V("qa", 0, P), V("sa", 0, P), V("xt", 0, 512))
-    pick(V("qs", 0, 64), V("ss", 0, 64), V("qa", 0, P), V("sa", 0, P), V("osd", 0, 4))
+    pick(V("qs", 0, K), V("ss", 0, K), V("qa", 0, P), V("sa", 0, P), V("osd", 0, 1))
     post_cols(0, "qs", "ss", 0)
 
-    for b in range(4):
+    pick(V("lq0", s0, s1), V("ls0", s0, s1), V("qa", 0, P), V("sa", 0, P), V("osd", 0, 1))
+    for b in range(3):
+        cp("s", V("et", 512 * b, 512 * b + 512), V("zt", 0, 512))
+    fill(V("et", 512 * 3, 512 * 4), 0.0)
+    turn(V("x2", 0, 32), V("cj0", 0, 32))
+    cp("v", V("li0", s0, s1), V("si0", 0, K))
+    cp("v", V("nbf", 0, 4), V("nbi", 0, 25, 8))
+    fill(V("rst", 0, SEG * P), 1.0)
+    ts(V("opm", 0, 8), V("c8", 0, 8), V("x2", 0, 1), A.subtract)
+    fill(V("z32", 0, 32), 0.0)
+    fill(V("zm0", P, P + 32), -BIG)
+    ts(V("e5", 0, SEG * P, SEG), row, -1472.0, A.add, UNIT, A.mult)
+    fill(V("rst", 0, SEG * P, SEG), 0.0)
+    for a in range(4):
+        ts(part(plc, 32 * a, 32 * a + 32), part(pcol, 32 * a, 32 * a + 32), 32.0 * (BLOCK[a] - a), A.add)
+    for b in (3, 0, 1, 2):
         ts(V("et", 512 * b + b, 512 * b + 512, 4), row, pcol, A.is_equal, 0.5, A.mult)
+    pick(V("qp", 0, P), V("sp", 0, P), V("qa", 0, P), V("sa", 0, P), V("opm", 0, 8))
     quant(V("qe", 0, 512), V("se", 0, 512), V("et", 0, 2048))
 
     def decode(qn, sn, c):
@@ -331,62 +370,55 @@ def rank_program(g, core, T, topo):
     def keep(b, at):
         cp("s", V("dec", 512 * b + at, 512 * b + at + P), V("db", 512 * b, 512 * b + P))
 
-    pick(V("lq0", s0, s1), V("ls0", s0, s1), V("qa", 0, P), V("sa", 0, P), V("osd", 0, 1))
     decode("qa", "sa", 0)
     for b in range(4):
         keep(b, 0)
-    cp("v", V("li0", s0, s1), V("si0", 0, K))
-    cp("v", V("nbf", 0, 4), V("nbi", 0, 25, 8))
-    fill(V("rst", 0, SEG * P), 1.0)
-    fill(V("z32", 0, 32), 0.0)
-    fill(V("zm0", P, P + 32), -BIG)
-    ts(V("e5", 0, SEG * P, SEG), row, -704.0, A.add, UNIT, A.mult)
-    fill(V("rst", 0, SEG * P, SEG), 0.0)
-    ts(V("ky0", KEYW - 1, KEYW), V("z32", 0, 1), -704.0 * UNIT, A.add)
+    ts(V("ky0", KEYW - 1, KEYW), V("z32", 0, 1), -960.0 * UNIT, A.add)
     cp("v", V("srow", 0, K), V("idtab", 0, P), V("osd", 0, 1))
     ts(V("x1", 0, 32), V("z32", 0, 32), pcol, A.add)
-    fill(V("pw", 0, 2 * P), -1.0)
-    ts(V("sm", 1, 2), pcol, g0, A.add)
-    spread_a("r1", "x1", 0)
+    ts(V("sm", 1, 2), plc, g0, A.add)
+    fill(V("ht", 4 * K, 512), 0.0)
+    turn(V("r1", 0, 32), V("x1", 0, 32))
     ts(V("val", 0, K), V("srow", 0, K), V("sm", 1, 2), A.is_equal)
-    spread_b("r1", "vvvv")
+    ts(V("tl", 0, 1), pcol, 64.0, A.is_lt, TINY, A.mult)
+    ts(V("tl", 1, 2), plc, 64.0, A.is_lt, -TINY, A.mult)
     red(V("sm", 0, 1), V("val", 0, K), A.max)
-    scatter(V("pw", 0, 2 * P), V("srow", 0, K), V("osd", 0, 1))
-    ts(V("th", 0, P), V("r1", 0, P), pcol, A.is_ge, -TINY, A.mult)
-    ts(V("thr", 0, 1), V("sm", 0, 1), 8.0, A.mult, -256.0 * UNIT, A.add)
-    ts(V("cc", 30, 31), pcol, 1024.0 / 2 ** 19, A.mult, 192.0 / 2 ** 19, A.add)
-    fill(V("ones", 0, P + 64), 1.0)
-    fill(V("cc", P + 32, P + 64), -1.0)
-    fill(V("ht", 0, 512), 0.0)
-    fill(V("cc", P + 32, P + 33), 0.0)
-    fill(V("cc", P + 32 + K, P + 33 + K), K - 1.0)
-    turn(V("x2", 0, 32), V("cj0", 0, 32))
+    ts(V("th", 0, 32), V("r1", 0, 32), pcol, A.is_ge, -TINY, A.mult)
+    for h, lift in enumerate((1472.0, 1280.0)):
+        ts(V("pc", h, h + 1), plc, 2048.0 * UNIT, A.mult, lift * UNIT, A.add)
+        ts(V("c4", 4 * h, 4 * h + 4), V("row", 0, 4), 0.5, A.mult, -lift * UNIT, A.add)
+    ts(V("thr", 0, 1), V("sm", 0, 1), 8.0, A.mult, -1024.0 * UNIT, A.add)
+    fill(V("ca", 65, 97), 0.0)
+    ts(V("cb", 129, 161), V("z32", 0, 32), -1.0, A.add)
     ts(V("oid", 0, 1), V("x2", 0, 1), -1.0, A.mult)
+    ts(V("cb", 129, 161, K), V("row", 0, 2), K - 1.0, A.mult)
 
     def late_constants():
         fill(V("rst16", 0, P), 1.0)
         fill(V("dm", P, 2 * P), 0.0)
+        fill(V("yw", pw, pw + P), -1.0)
         for a in range(4):
             ts(V("dm", 32 * a, 32 * a + 32), V("cj0", 0, 32), V("x2", 0, 1), A.is_equal)
         fill(V("rst16", 0, P, 16), 0.0)
+        scatter(V("yw", pw, pw + P), V("srow", 0, K), V("osd", 0, 1))
         tt(V("mp", 0, P), V("dm", 0, P), row, A.mult)
 
     def products_w(c):
         for o in range(O):
             mm(V("yb", 512 * o, 512 * o + P), V("qw", P * o, P * o + P), V("sw", P * o, P * o + P), V("qa", c, c + P), V("sa", c, c + P))
 
-    def y_out(o):
-        cp("s", V("yn", K * o, K * o + K), V("yb", 512 * o, 512 * o + K))
-
-    def y_put(o, hi):
-        scatter(V("yw", 2 * P * o, 2 * P * o + 2 * P), V("yn", K * o, K * o + K), hi)
+    def new_y(t):
+        products_w(P * (t + 1))
+        for o in range(O):
+            cp("s", V("yn%d" % t, K * o, K * o + K), V("yb", 512 * o, 512 * o + K))
 
     for t in range(R):
         li, lq, ls = V("li%d" % t, 0, P), V("lq%d" % t, 0, P), V("ls%d" % t, 0, P)
-        ky, kn, zm, zn = "ky%d" % t, "ky%d" % (t + 1), "zm%d" % t, "zm%d" % (t + 1)
-        best, km, ib = V("bs", P, P + 1), V(kn, KEYW - 1, KEYW), V("cc", 31, 32)
-        hi, lo = V("of%d" % t, 0, 1), V("of%d" % t, 2, 3)
+        ky, kn, zm, zn, yn = "ky%d" % t, "ky%d" % (t + 1), "zm%d" % t, "zm%d" % (t + 1), "yn%d" % t
+        best, km, ib = V("bs", 64, 65), V("cb", 64, 65), V("ca", 0, 1)
+        hi, hi4, lo = V("of%d" % t, 0, 1), V("of%d" % t, 0, 4), V("of%d" % t, 4, 5)
         last = t + 1 == R
+        h = int(last)
         c = P * (t + 1)
         for k in range(M):
             ts(V("e5", 1 + k, SEG * P, SEG), li, V("nbf", k, k + 1), A.is_equal, 512.0 * (M - k) * UNIT, A.mult)
@@ -394,35 +426,47 @@ def rank_program(g, core, T, topo):
         ts(V("am", 0, P), V(ky, M, SEG * P, SEG), V("thr", 0, 1), A.is_lt, -BIG, A.mult)
         if last:
             cp("v", V("lif", P * t, P * t + P), li)
-        mm(V("zb", 0, P), V("qa", 0, P), V("sa", 0, P), lq, ls)
+        mm(V("zb", 0, P), V("qp", 0, P), V("sp", 0, P), lq, ls)
         decode(lq[0], ls[0], 0)
         tt(V(zm, 0, P), V("zb", 0, P), V("am", 0, P), A.add)
-        scan(V("bs", 0, P + 32), V(zm, 0, P + 32), V(zm, 0, P + 32), -2.0 * BIG, A.max, A.max)
+        scan(V("bs", 0, 96), V(zm, 0, 96), V(zm, 64, 160), -2.0 * BIG, A.max, A.max)
         act(V("pen", 0, P + 1), V(zm, 0, P + 1), SIGN, best)
-        spread_a("r1", "bs", P)
-        spread_b("r1", "ssss")
-        act(V("dd", 0, P), V("r1", 0, P), SAME, best)
-        for b in range(4):
+        turn(V("r1", 0, 32), V("bs", 64, 96))
+        turn(V("r1", 32, 64, 1, 0, 64), V("bs", 64, 96, 1, 64, 128))
+        turn(V("r1", 32, 64, 1, 64, 128), V("bs", 64, 96, 1, 0, 64))
+        for a in range(4):
+            b = a ^ 1
+            act(V("dd", 32, 96, 1, 32 * a, 32 * a + 32), V("r1", 0, 64, 1, 32 * b, 32 * b + 32), SAME, part(best, 32 * a, 32 * a + 32))
+        act(V("dd", 0, 32), V("r1", 0, 32), SAME, best)
+        issue("s", lambda e, ib=ib, best=best: e.activation(ap(ib), ap(best), RELU, scale=-0.25 / BIG), [ib], [best])
+        for b in range(3):
             keep(b, c)
         tt(V("kp", 0, P + 1), V(ky, M, KEYW, SEG), V("pen", 0, P + 1), A.subtract)
-        ts(ib, best, -0.1 * BIG, A.is_lt, 0.25, A.mult)
-        scan(V(kn, KEYW - P - 1, KEYW), V("kp", 0, P + 1), V("kp", 0, P + 1), -2.0, A.max, A.max)
-        ts(V("sm", 3, 4), km, 1.5 * 2 ** 20, A.add, 1.5 * 2 ** 20, A.subtract)
-        tt(V("cc", 32, P + 32), V("dd", 0, P), V("th", 0, P), A.is_le)
-        ts(V("sm", 4, 5), km, V("sm", 3, 4), A.subtract, 2.0 ** -7, A.mult)
-        scan(V("u1", 30, P + 64), V("ones", 30, P + 64), V("cc", 30, P + 64), V("sm", 4, 5))
-        u1 = V("u1", P + 31, P + 32)
-        spread_a("r2", "u1", P + 32)
-        spread_b("r2", "vsvs")
-        red(V("sm", 5, 6), V("r2", 0, P), A.min, True)
-        ts(hi, V("sm", 5, 6), 512.0, A.mult)
-        ts(V("sm", 6, 7), V("sm", 5, 6), 1.5 * 2 ** 14, A.add, 1.5 * 2 ** 14, A.subtract)
+        ts(V("ca", 33, 65), V("r1", 32, 64), best, A.subtract, V("tl", 0, 1), A.is_ge)
+        scan(V("cb", 0, 65), V("kp", 0, 65), V("kp", 64, 129), -2.0, A.max, A.max)
+        ts(V("cb", 65, 129), V("dd", 32, 96), V("tl", 1, 2), A.is_le)
+        tt(V("ca", 1, 33), V("dd", 0, 32), V("th", 0, 32), A.is_le)
+        scan(V("u1", 0, 97), V("ca", 0, 97), V("cb", 64, 161), V("pc", h, h + 1), A.add, A.add)
+        u1 = V("u1", 64, 65)
+        turn(V("r2", 0, 32), V("u1", 65, 97))
+        turn(V("r2", 32, 64, 1, 0, 64), V("u1", 65, 97, 1, 64, 128))
+        turn(V("r2", 32, 64, 1, 64, 128), V("u1", 65, 97, 1, 0, 64))
+        for a in range(4):
+            b = a ^ 1
+            cp("vsvs"[a], V("r2", 64, 128, 1, 32 * a, 32 * a + 32), V("r2", 0, 64, 1, 32 * b, 32 * b + 32))
+        keep(3, c)
+        won = V("sm", 5, 6)
+        red(won, V("r2", 0, P), A.min, True)
+        ts(hi4, V("c4", 4 * h, 4 * h + 4), won, A.add, 512.0, A.mult)
+        ts(V("sm", 6, 7), won, 1.5 * 2 ** 12, A.add, 1.5 * 2 ** 12, A.subtract)
         if not last:
             cp("v", V("si%d" % (t + 1), 0, K), V("idtab", 0, 2 * P), hi)
             post_ids(t + 1)
+            ts(lo, won, V("sm", 6, 7), A.subtract, 1.0 / UNIT, A.mult)
         else:
+            ts(V("sm", 3, 4), won, 1.0 / UNIT, A.mult, 192.0, A.add)
             tt(V("val", 0, K), V("dm", 0, 2 * P), V("vr", 0, K), A.mult, hi)
-        ts(lo, V("sm", 5, 6), V("sm", 6, 7), A.subtract, 2.0 ** 19, A.mult)
+            ts(lo, V("sm", 6, 7), -1.0 / UNIT, A.mult, V("sm", 3, 4), A.add)
         for b in range(4):
             cp("s", V("go", K * b, K * b + K), V("dec", 512 * b, 512 * b + 2 * P), hi)
         for b in range(4):
@@ -433,50 +477,47 @@ def rank_program(g, core, T, topo):
         if not last:
             post_cols(t + 1, "qa", "sa", c)
             pick(V("lq%d" % (t + 1), s0, s1), V("ls%d" % (t + 1), s0, s1), V("qa", c, c + P), V("sa", c, c + P), V("oid", 0, 1))
-            cp("v", V("li%d" % (t + 1), s0, s1), V("si%d" % (t + 1), 0, K))
-            ts(V("e5", 0, SEG * P, SEG), row, float(c) - 704.0, A.add, UNIT, A.mult)
-            ts(V("sm", 7, 8), ib, 100.0, A.mult, u1, A.add)
-            fill(V(zn, P + 1, P + 32), -BIG)
-            ts(V("sm", 8, 9), V("sm", 7, 8), float(K), A.is_lt, 8.0, A.mult)
-            tt(V("thr", 0, 1), V("thr", 0, 1), V("sm", 8, 9), A.add)
-            ts(V("sm", 9, 10), V("thr", 0, 1), 1.0, A.is_lt, 2.0 * BIG, A.mult)
-            ts(V(zn, P, P + 1), V("sm", 9, 10), -BIG, A.add, best, A.min)
-            if t == 0:
+            if t == 1:
                 quant(V("qw", 0, P * O), V("sw", 0, P * O), V("wt", 0, 512 * O))
-                late_constants()
                 products_w(0)
                 for o in range(O):
                     cp("s", V("yw", 2 * P * o, 2 * P * o + P), V("yb", 512 * o, 512 * o + P))
-                ts(V("vr", 0, K), V("row", 0, K), float(c), A.add)
+                new_y(0)
+                new_y(1)
+            cp("v", V("li%d" % (t + 1), s0, s1), V("si%d" % (t + 1), 0, K))
+            ts(V("e5", 0, SEG * P, SEG), row, float(c) - 1472.0, A.add, UNIT, A.mult)
+            ts(V("sm", 7, 8), ib, 100.0, A.mult, u1, A.add)
+            fill(V(zn, P + 1, P + 32), -BIG)
+            ts(V("sm", 8, 9), V("sm", 7, 8), float(K), A.is_lt, 8.0, A.mult)
+            cp("v", V(kn, KEYW - 1, KEYW), km)
+            tt(V("thr", 0, 1), V("thr", 0, 1), V("sm", 8, 9), A.add)
             cp("v", V("lif", P * t, P * t + P), li)
-        products_w(c)
-        cp("s", V("pr", 0, K), V("lif", 0, c), lo)
-        if not last:
+            ts(V("sm", 9, 10), V("thr", 0, 1), 1.0, A.is_lt, 2.0 * BIG, A.mult)
+            ts(V("vr", 0, K), V("row", 0, K), float(c), A.add)
+            ts(V(zn, P, P + 1), V("sm", 9, 10), -BIG, A.add, best, A.min)
+            if t == 0:
+                late_constants()
+            cp("s", V(yn, K * O, K * O + K), V("lif", 0, c), lo)
             tt(V("val", 0, K), V("dm", 0, 2 * P), V("vr", 0, K), A.mult, hi)
             scatter(V("mp", 0, 2 * P), V("val", 0, K), hi)
-            for o in range(O):
-                y_out(o)
-                y_put(o, hi)
-            scatter(V("pw", 0, 2 * P), V("pr", 0, K), hi)
-            ts(V("vr", 0, K), V("row", 0, K), float(c + P), A.add)
+            if t == 1:
+                ts(V("vr", 0, K), V("row", 0, K), float(c + P), A.add)
+                for u in range(2):
+                    scatter(V("yw", 0, pw + 2 * P), V("yn%d" % u, 0, K * O + K), V("of%d" % u, 0, 4))
         else:
+            cp("s", V(yn, K * O, K * O + K), V("lif", 0, c), lo)
+            new_y(t)
             scan(V("mps", 0, P), V("rst16", 0, P), V("mp", 0, P), 0.0)
-            scatter(V("pw", 0, 2 * P), V("pr", 0, K), hi)
-            dma("y", "d_out", T.pa[:], T.pw[0:1, 0:P], [], [V("pw", 0, P)])
             cp("v", V("omap", 0, 8), V("mps", 15, P, 16))
-            y_out(0)
+            for o in range(O):
+                scatter(V("yw", 2 * P * o, 2 * P * o + 2 * P), V(yn, K * o, K * o + K), hi)
+                dma("y", "d_out", T.y[:, P * o:P * o + P], T.yw[:, 2 * P * o:2 * P * o + P], [], [V("yw", 2 * P * o, 2 * P * o + P)])
             pick(V("qf", 0, P), V("sf", 0, P), V("qa", 0, 512), V("sa", 0, 512), V("omap", 0, 8))
-            y_out(1)
-            y_out(2)
             dma("y", "d_out", T.oc[:], T.qf[:, 0:P].bitcast(dt.uint8), [], [V("qf", 0, P)])
-            y_put(0, hi)
-            dma("y", "d_out", T.y[:, 0:P], T.yw[:, 0:P], [], [V("yw", 0, P)])
-            y_put(1, hi)
-            dma("y", "d_out", T.y[:, P:2 * P], T.yw[:, 2 * P:3 * P], [], [V("yw", 2 * P, 3 * P)])
+            scatter(V("yw", pw, pw + 2 * P), V(yn, K * O, K * O + K), hi)
             for a in range(4):
                 dma("s", "d_out", T.osc[4 * a:4 * a + 4, 0:P], T.sf[32 * a:32 * a + 4, 0:P], [], [V("sf", 0, P)])
-            y_put(2, hi)
-            dma("y", "d_out", T.y[:, 2 * P:3 * P], T.yw[:, 4 * P:5 * P], [], [V("yw", 4 * P, 5 * P)])
+            dma("y", "d_out", T.pa[:], T.yw[0:1, pw:pw + P], [], [V("yw", pw, pw + P)])
 
     value = {}
     run = {q: 0 for q in eng}

from concourse.bass import DstId, RemoteDMATransfer
from concourse.mybir import dt, AluOpType, AxisListType, ActivationFunctionType

P, K, R, M, O = 128, 16, 3, 4, 3
SEG = M + 1
KEYW = SEG * (P + 1)
BIG = 2.0 ** 96
TINY = 1.0e-37
UNIT = 2.0 ** -20
BLOCK = (0, 2, 1, 3)
F32, BF16, F16, I32, U16, U8, CODE = "float32", "bfloat16", "float16", "int32", "uint16", "uint8", "float8_e4m3fn_x4"


def _sb(n, d):
    return ("sbuf", [128, n], d)


SCRATCH = {
    "xt": _sb(4 * P, BF16), "wt": _sb(512 * O, BF16), "et": _sb(2048, BF16), "ht": _sb(512, BF16), "zt": _sb(512, BF16),
    "qa": _sb(512, CODE), "sa": _sb(512, U8), "qw": _sb(P * O, CODE), "sw": _sb(P * O, U8),
    "qe": _sb(512, CODE), "se": _sb(512, U8), "qs": _sb(P + K, CODE), "ss": _sb(P + K, U8),
    "qf": _sb(P, CODE), "sf": _sb(P, U8), "qp": _sb(P, CODE), "sp": _sb(P, U8),
    "sdi": _sb(4, I32), "nbi": _sb(32, I32), "nbf": _sb(4, F32), "osd": _sb(4, U16), "oid": _sb(2, U16), "omap": _sb(8, U16),
    "opm": _sb(8, U16), "c8": _sb(8, F32), "plc": _sb(1, F32),
    "pcol": _sb(1, F32), "row": _sb(P, F32), "idtab": _sb(2 * P, F32), "cj0": _sb(32, F32), "z32": _sb(32, F32),
    "th": _sb(32, F32), "tl": _sb(2, F32), "rst": _sb(SEG * P, BF16), "rst16": _sb(P, F32), "e5": _sb(SEG * P, F16),
    "am": _sb(P, BF16), "pen": _sb(P + 2, BF16), "kp": _sb(P + 2, F16), "x1": _sb(32, F32), "x2": _sb(32, F32), "thr": _sb(1, F32),
    "r1": _sb(64, F32), "r2": _sb(P, F32), "dd": _sb(96, F32), "ca": _sb(98, BF16), "cb": _sb(162, F16), "u1": _sb(97, F32),
    "bs": _sb(96, F32), "pc": _sb(2, F32), "c4": _sb(8, F32),
    "sm": _sb(16, F32), "go": _sb(64, BF16), "dec": _sb(2048, BF16),
    "srow": _sb(K, F32), "lif": _sb(P * R, F32),
    "dm": _sb(2 * P, F32), "mp": _sb(2 * P, F32), "mps": _sb(P, F32), "vr": _sb(K, F32), "val": _sb(K, F32),
    "yw": _sb(2 * P * (O + 1), F32),
    "zb": ("psum", [128, 512], F32), "db": ("psum", [128, 2048], F32), "yb": ("psum", [128, 512 * O], F32),
}
for _t in range(R):
    SCRATCH["lq%d" % _t] = _sb(P, CODE)
    SCRATCH["ls%d" % _t] = _sb(P, U8)
    SCRATCH["li%d" % _t] = _sb(P, U16)
    SCRATCH["si%d" % _t] = _sb(K, U16)
    SCRATCH["rq%d" % _t] = _sb(K, CODE)
    SCRATCH["rs%d" % _t] = _sb(4 * K, U8)
    SCRATCH["ri%d" % _t] = _sb(K, U16)
    SCRATCH["of%d" % _t] = _sb(6, U16)
    SCRATCH["zm%d" % _t] = _sb(P + 32, F32)
    SCRATCH["ky%d" % _t] = _sb(KEYW + 3, F16)
    SCRATCH["yn%d" % _t] = _sb(K * (O + 1), F32)

SEMAPHORES = ["c_v", "c_s", "c_t", "c_g", "d_x", "d_sd", "d_nb", "d_w", "d_out", "gone"] + \
    ["ai%d" % t for t in range(R)] + ["ac%d" % t for t in range(R)]

A = AluOpType
COPY = ActivationFunctionType.Copy
SIGN = ActivationFunctionType.Sign
SAME = ActivationFunctionType.Identity
RELU = ActivationFunctionType.Relu
CODES, SCALES, IDS = 0, 1, 2


def V(name, c0, c1, step=1, p0=0, p1=128):
    return (name, c0, c1, step, p0, p1)


def _meet(a, b, other_queue):
    if a[0] != b[0]:
        return False
    if SCRATCH[a[0]][0] == "psum" and other_queue:
        return a[1] // 512 <= (b[2] - 1) // 512 and b[1] // 512 <= (a[2] - 1) // 512
    if a[4] >= b[5] or b[4] >= a[5] or a[1] >= b[2] or b[1] >= a[2]:
        return False
    if a[3] == b[3] and a[3] > 1 and (a[1] - b[1]) % a[3]:
        return False
    return True


def _mask(engines):
    m = 0
    for e in engines:
        m |= 1 << e
    return m


def _dst(topo, dst, src):
    rid, pid = topo.addr(dst, src)
    return DstId(rid=rid, pnc=pid)


def _common(topo, src, cores):
    es = topo.engines(src, cores[0])
    return [e for e in es if all(e in topo.engines(src, c) for c in cores)]


def _routes(T, topo, rank):
    me = T.cores[rank]
    n = len(T.cores)
    ring = [(rank + i) % n for i in range(1, n)]
    near = [q for q in ring if topo.may_write(me, T.cores[q])]
    far = [q for q in ring if q not in near]
    free = sorted([c for c in topo.cores_of(me) if c not in T.cores], key=lambda c: (topo.die(c) != topo.die(me), c))
    able = [c for c in free if all(topo.may_write(c, T.cores[q]) for q in far)]
    out = _common(topo, me, [T.cores[q] for q in near])
    every = _common(topo, me, free)
    home = [e for e in every if e not in out]
    e4 = [every[4 * i:4 * i + 4] for i in range(4)]
    straight = [(T.cores[q], None) for q in near]
    ids = [[(IDS, home[:4], [(able[1], far[:2])]), (IDS, home[4:], [(able[3], far[2:])]), (IDS, out, straight)]]
    cols = [[(CODES, e4[2], [(able[0], far[:2])]), (CODES, e4[3], [(able[2], far[2:])]),
             (SCALES, e4[0], [(able[1], far[:2])]), (SCALES, e4[1], [(able[3], far[2:])])],
            [(CODES, out, straight)], [(SCALES, out, straight)]]
    return ids, cols


def relay_program(g, core, T, topo, rank, routes):
    a, b = K * rank, K * rank + K
    gone = 0
    for t in range(R):
        for calls in routes:
            for call in calls:
                for piece, given, targets in call:
                    for c, dests in targets:
                        if c != core:
                            continue
                        cores = [T.cores[q] for q in dests]
                        es = _common(topo, core, cores)
                        if piece == IDS:
                            sem, src, dst = "ai%d" % t, T["ri%d" % t][:, 0:K], T["li%d" % t][:, a:b]
                        elif piece == CODES:
                            sem = "ac%d" % t
                            src, dst = T["rq%d" % t][:, 0:K].bitcast(dt.uint8), T["lq%d" % t][:, a:b].bitcast(dt.uint8)
                        else:
                            sem, src, dst = "ac%d" % t, T["rs%d" % t][:, 0:K], T["ls%d" % t][:, a:b]
                        g.wait_ge(T.sem[sem], len(given))
                        g.remote_dma_fused([RemoteDMATransfer(dst_ids=[_dst(topo, u, core) for u in cores],
                                                              dma_engine_mask=_mask(es), remote_sem=T.sem[sem], srcs=[src],
                                                              dsts=[dst for u in cores])], local_sem=T.sem.gone)
                        gone += len(es)
    if gone:
        g.wait_ge(T.sem.gone, gone)


def rank_program(g, core, T, topo):
    rank = T.rank_of(core)
    N = len(T.cores)
    if rank is None:
        for r in range(N):
            relay_program(g, core, T, topo, r, _routes(T, topo, r))
        return
    routes = _routes(T, topo, rank)
    eng = {"v": g.vector, "s": g.scalar, "t": g.tensor, "g": g, "y": g.sync}
    ops = []
    hist = []
    clock = {q: {} for q in eng}
    known = {}
    count = {q: 0 for q in eng}
    total = {}
    waited = set()

    def ap(v):
        if v[3] == 1:
            return T[v[0]][v[4]:v[5], v[1]:v[2]]
        return T[v[0]][v[4]:v[5], v[1]:v[2]:v[3]]

    def issue(q, call, outs, ins, sem=None, track=True):
        need = []
        for view, wr, q2, tok in hist:
            psum = SCRATCH[view[0]][0] == "psum" and q2 != q
            hit = any(_meet(view, o, q2 != q) for o in outs) or ((wr or psum) and any(_meet(view, i, q2 != q) for i in ins))
            if hit and tok not in need and (sem is None or tok[0] != sem):
                need.append(tok)
        need.sort(key=lambda k: -k[1])
        waits = []
        for tok in need:
            if any(tok != o and known[o].get(tok[0], 0) >= tok[1] for o in need):
                continue
            if clock[q].get(tok[0], 0) < tok[1]:
                waits.append(tok)
                waited.add(tok)
                for k, n in known[tok].items():
                    clock[q][k] = max(clock[q].get(k, 0), n)
        if sem is None:
            count[q] += 1
            tok = (q, count[q])
        else:
            tok = (sem, 1)
            total[sem] = total.get(sem, 0) + 16
        if track:
            k = dict(clock[q])
            if tok in known:
                k = {a: min(n, known[tok].get(a, 0)) for a, n in k.items()}
            k[tok[0]] = tok[1]
            known[tok] = k
            for o in outs:
                hist.append((o, True, q, tok))
            for i in ins:
                hist.append((i, False, q, tok))
        ops.append((q, call, waits, tok if track else None, sem))

    def arrival(sem, n, outs):
        total[sem] = n
        known[(sem, 1)] = {sem: 1}
        for o in outs:
            hist.append((o, True, "far", (sem, 1)))

    def views(*xs):
        return [x for x in xs if isinstance(x, tuple)]

    def arg(x):
        return ap(x) if isinstance(x, tuple) else x

    def part(v, p0, p1):
        return v[:4] + (p0, p1)

    def ts(out, in0, s1, op0, s2=None, op1=None):
        if op1 is None:
            issue("v", lambda e: e.tensor_scalar(ap(out), ap(in0), arg(s1), None, op0), [out], views(in0, s1))
        else:
            issue("v", lambda e: e.tensor_scalar(ap(out), ap(in0), arg(s1), arg(s2), op0, op1), [out], views(in0, s1, s2))

    def tt(out, in0, in1, op, off=None):
        if off is None:
            issue("v", lambda e: e.tensor_tensor(ap(out), ap(in0), ap(in1), op), [out], [in0, in1])
        else:
            issue("v", lambda e: e.tensor_tensor(ap(out), ap(in0).indirect(ap(off)), ap(in1), op), [out], [in0, in1, off])

    def cp(q, out, in_, off=None):
        ins = [in_] if off is None else [in_, off]
        src = (lambda: ap(in_)) if off is None else (lambda: ap(in_).indirect(ap(off)))
        if q == "v":
            issue("v", lambda e: e.tensor_copy(ap(out), src()), [out], ins)
        else:
            issue("s", lambda e: e.activation(ap(out), src(), COPY), [out], ins)

    def pick(qo, so, qi, si, off):
        issue("v", lambda e: e.tensor_copy(ap(qo).bitcast(dt.uint32), ap(qi).bitcast(dt.uint32).indirect(ap(off))), [qo], [qi, off])
        cp("s", so, si, off)

    def act(out, in_, func, bias):
        issue("s", lambda e: e.activation(ap(out), ap(in_), func, bias=ap(bias), scale=-1.0), [out], [in_, bias])

    def scatter(win, vals, off):
        issue("v", lambda e: e.tensor_copy(ap(win).indirect(ap(off)), ap(vals)), [win], [vals, off])

    def red(out, in_, op, absolute=False):
        if absolute:
            issue("v", lambda e: e.tensor_reduce(ap(out), ap(in_), AxisListType.X, op, apply_absolute_value=True), [out], [in_])
        else:
            issue("v", lambda e: e.tensor_reduce(ap(out), ap(in_), AxisListType.X, op), [out], [in_])

    def scan(out, d0, d1, init, op0=A.mult, op1=A.add):
        issue("v", lambda e: e.tensor_tensor_scan(ap(out), ap(d0), ap(d1), arg(init), op0, op1), [out], views(d0, d1, init))

    def fill(out, c):
        issue("v", lambda e: e.memset(ap(out), c), [out], [])

    def quant(q, s, in_):
        issue("v", lambda e: e.quantize_mx(ap(q), ap(s), ap(in_)), [q, s], [in_])

    def mm(out, wq, ws, xq, xs):
        issue("t", lambda e: e.matmul_mx(ap(out), ap(wq), ap(ws), ap(xq), ap(xs), True, True), [out], [wq, ws, xq, xs])

    def turn(out, in_):
        issue("v", lambda e: e.transpose(ap(out), ap(in_)), [out], [in_])

    def dma(q, sem, out, in_, outs, ins):
        issue(q, lambda e: e.dma_start(out, in_), outs, ins, sem=sem)

    def iota(out, pattern, mult):
        issue("g", lambda e: e.iota(ap(out), pattern, 0, mult, allow_small_or_imprecise_dtypes=True), [out], [])

    sent = [0]
    s0, s1 = K * rank, K * rank + K

    def post(calls, t, qn, sn, c0):
        for call in calls:
            wide = any(piece == CODES for piece, es, targets in call)
            xs, ins = [], []
            for piece, es, targets in call:
                if piece == IDS:
                    v, sem = V("si%d" % t, 0, K), "ai%d" % t
                    src, mid, end = ap(v), T["ri%d" % t][:, 0:K], T["li%d" % t][:, s0:s1]
                elif piece == CODES:
                    v, sem = V(qn, c0, c0 + K), "ac%d" % t
                    src = ap(v).bitcast(dt.uint8)
                    mid, end = T["rq%d" % t][:, 0:K].bitcast(dt.uint8), T["lq%d" % t][:, s0:s1].bitcast(dt.uint8)
                else:
                    n = 4 * K if wide else K
                    v, sem = V(sn, c0, c0 + n), "ac%d" % t
                    src, mid, end = ap(v), T["rs%d" % t][:, 0:n], T["ls%d" % t][:, s0:s1]
                sent[0] += len(es)
                ins.append(v)
                xs.append(RemoteDMATransfer(dst_ids=[_dst(topo, c, core) for c, d in targets], dma_engine_mask=_mask(es),
                                            remote_sem=T.sem[sem], srcs=[src],
                                            dsts=[end if d is None else mid for c, d in targets]))
            issue("g", lambda e, xs=xs: e.remote_dma_fused(xs, local_sem=T.sem.gone), [], ins, track=False)

    def post_ids(t):
        post(routes[0], t, None, None, 0)

    def post_cols(t, qn, sn, c0):
        post(routes[1], t, qn, sn, c0)

    n_arr = [0, 0, 0]
    for q in range(N):
        for calls in _routes(T, topo, q):
            for call in calls:
                for piece, es, targets in call:
                    for c, dests in targets:
                        if dests is None:
                            n_arr[piece] += len(es) if c == core else 0
                        elif rank in dests:
                            n_arr[piece] += len(_common(topo, c, [T.cores[u] for u in dests]))
    others = [(K * q, K * q + K) for q in range(N) if q != rank]
    for t in range(R):
        arrival("ai%d" % t, n_arr[IDS], [V("li%d" % t, a, b) for a, b in others])
        arrival("ac%d" % t, n_arr[CODES] + n_arr[SCALES], [V(n % t, a, b) for a, b in others for n in ("lq%d", "ls%d")])

    pcol, plc = V("pcol", 0, 1), V("plc", 0, 1)
    row = V("row", 0, P)
    g0 = float(P * rank)
    pw = 2 * P * O

    for h in range(2):
        dma("s", "d_sd", T.sdi[16 * h:16 * h + 16, 0:1], T.sd[:], [V("sdi", 0, 1, 1, 16 * h, 16 * h + 16)], [])
    dma("y", "d_x", T.xt[:], T.x[:], [V("xt", 0, 512)], [])
    for h in range(8):
        u = 2 * BLOCK[h // 2] + h % 2
        dma("y", "d_nb", T.nbi[16 * h:16 * h + 16, 0:25], T.nb[:, u:u + 25], [V("nbi", 0, 25, 1, 16 * h, 16 * h + 16)], [])
    dma("y", "d_w", T.wt[:], T.w[:], [V("wt", 0, 512 * O)], [V("li0", others[0][0], others[0][1])])

    iota(row, [[1, P]], 0)
    iota(pcol, [[1, 1]], 1)
    iota(V("cj0", 0, 32), [[0, 2], [-1, 16]], 0)
    iota(V("c8", 0, 8), [[32 * BLOCK[2], 2], [32 * BLOCK[1], 2], [16, 2]], 0)
    fill(V("zt", 0, 512), 0.0)
    fill(V("idtab", P, 2 * P), 4000.0)
    quant(V("qs", K, K + P), V("ss", K, K + P), V("zt", 0, 512))
    ts(V("idtab", 0, P), row, g0, A.add)
    for a in range(4):
        cp("v", V("osd", 0, 1, 1, 32 * a, 32 * a + 32), V("sdi", 0, 1, 1, 0, 32))
    cp("v", V("si0", 0, K), V("idtab", 0, 2 * P), V("osd", 0, 1))
    post_ids(0)
    quant(V("qa", 0, P), V("sa", 0, P), V("xt", 0, 512))
    pick(V("qs", 0, K), V("ss", 0, K), V("qa", 0, P), V("sa", 0, P), V("osd", 0, 1))
    post_cols(0, "qs", "ss", 0)

    pick(V("lq0", s0, s1), V("ls0", s0, s1), V("qa", 0, P), V("sa", 0, P), V("osd", 0, 1))
    for b in range(3):
        cp("s", V("et", 512 * b, 512 * b + 512), V("zt", 0, 512))
    fill(V("et", 512 * 3, 512 * 4), 0.0)
    turn(V("x2", 0, 32), V("cj0", 0, 32))
    cp("v", V("li0", s0, s1), V("si0", 0, K))
    cp("v", V("nbf", 0, 4), V("nbi", 0, 25, 8))
    fill(V("rst", 0, SEG * P), 1.0)
    ts(V("opm", 0, 8), V("c8", 0, 8), V("x2", 0, 1), A.subtract)
    fill(V("z32", 0, 32), 0.0)
    fill(V("zm0", P, P + 32), -BIG)
    ts(V("e5", 0, SEG * P, SEG), row, -1472.0, A.add, UNIT, A.mult)
    fill(V("rst", 0, SEG * P, SEG), 0.0)
    for a in range(4):
        ts(part(plc, 32 * a, 32 * a + 32), part(pcol, 32 * a, 32 * a + 32), 32.0 * (BLOCK[a] - a), A.add)
    for b in (3, 0, 1, 2):
        ts(V("et", 512 * b + b, 512 * b + 512, 4), row, pcol, A.is_equal, 0.5, A.mult)
    pick(V("qp", 0, P), V("sp", 0, P), V("qa", 0, P), V("sa", 0, P), V("opm", 0, 8))
    quant(V("qe", 0, 512), V("se", 0, 512), V("et", 0, 2048))

    def decode(qn, sn, c):
        for b in range(4):
            mm(V("db", 512 * b, 512 * b + P), V("qe", P * b, P * b + P), V("se", P * b, P * b + P), V(qn, c, c + P), V(sn, c, c + P))

    def keep(b, at):
        cp("s", V("dec", 512 * b + at, 512 * b + at + P), V("db", 512 * b, 512 * b + P))

    decode("qa", "sa", 0)
    for b in range(4):
        keep(b, 0)
    ts(V("ky0", KEYW - 1, KEYW), V("z32", 0, 1), -960.0 * UNIT, A.add)
    cp("v", V("srow", 0, K), V("idtab", 0, P), V("osd", 0, 1))
    ts(V("x1", 0, 32), V("z32", 0, 32), pcol, A.add)
    ts(V("sm", 1, 2), plc, g0, A.add)
    fill(V("ht", 4 * K, 512), 0.0)
    turn(V("r1", 0, 32), V("x1", 0, 32))
    ts(V("val", 0, K), V("srow", 0, K), V("sm", 1, 2), A.is_equal)
    ts(V("tl", 0, 1), pcol, 64.0, A.is_lt, TINY, A.mult)
    ts(V("tl", 1, 2), plc, 64.0, A.is_lt, -TINY, A.mult)
    red(V("sm", 0, 1), V("val", 0, K), A.max)
    ts(V("th", 0, 32), V("r1", 0, 32), pcol, A.is_ge, -TINY, A.mult)
    for h, lift in enumerate((1472.0, 1280.0)):
        ts(V("pc", h, h + 1), plc, 2048.0 * UNIT, A.mult, lift * UNIT, A.add)
        ts(V("c4", 4 * h, 4 * h + 4), V("row", 0, 4), 0.5, A.mult, -lift * UNIT, A.add)
    ts(V("thr", 0, 1), V("sm", 0, 1), 8.0, A.mult, -1024.0 * UNIT, A.add)
    fill(V("ca", 65, 97), 0.0)
    ts(V("cb", 129, 161), V("z32", 0, 32), -1.0, A.add)
    ts(V("oid", 0, 1), V("x2", 0, 1), -1.0, A.mult)
    ts(V("cb", 129, 161, K), V("row", 0, 2), K - 1.0, A.mult)

    def late_constants():
        fill(V("rst16", 0, P), 1.0)
        fill(V("dm", P, 2 * P), 0.0)
        fill(V("yw", pw, pw + P), -1.0)
        for a in range(4):
            ts(V("dm", 32 * a, 32 * a + 32), V("cj0", 0, 32), V("x2", 0, 1), A.is_equal)
        fill(V("rst16", 0, P, 16), 0.0)
        scatter(V("yw", pw, pw + P), V("srow", 0, K), V("osd", 0, 1))
        tt(V("mp", 0, P), V("dm", 0, P), row, A.mult)

    def products_w(c):
        for o in range(O):
            mm(V("yb", 512 * o, 512 * o + P), V("qw", P * o, P * o + P), V("sw", P * o, P * o + P), V("qa", c, c + P), V("sa", c, c + P))

    def new_y(t):
        products_w(P * (t + 1))
        for o in range(O):
            cp("s", V("yn%d" % t, K * o, K * o + K), V("yb", 512 * o, 512 * o + K))

    for t in range(R):
        li, lq, ls = V("li%d" % t, 0, P), V("lq%d" % t, 0, P), V("ls%d" % t, 0, P)
        ky, kn, zm, zn, yn = "ky%d" % t, "ky%d" % (t + 1), "zm%d" % t, "zm%d" % (t + 1), "yn%d" % t
        best, km, ib = V("bs", 64, 65), V("cb", 64, 65), V("ca", 0, 1)
        hi, hi4, lo = V("of%d" % t, 0, 1), V("of%d" % t, 0, 4), V("of%d" % t, 4, 5)
        last = t + 1 == R
        h = int(last)
        c = P * (t + 1)
        for k in range(M):
            ts(V("e5", 1 + k, SEG * P, SEG), li, V("nbf", k, k + 1), A.is_equal, 512.0 * (M - k) * UNIT, A.mult)
        scan(V(ky, 0, SEG * P), V("rst", 0, SEG * P), V("e5", 0, SEG * P), 0.0)
        ts(V("am", 0, P), V(ky, M, SEG * P, SEG), V("thr", 0, 1), A.is_lt, -BIG, A.mult)
        if last:
            cp("v", V("lif", P * t, P * t + P), li)
        mm(V("zb", 0, P), V("qp", 0, P), V("sp", 0, P), lq, ls)
        decode(lq[0], ls[0], 0)
        tt(V(zm, 0, P), V("zb", 0, P), V("am", 0, P), A.add)
        scan(V("bs", 0, 96), V(zm, 0, 96), V(zm, 64, 160), -2.0 * BIG, A.max, A.max)
        act(V("pen", 0, P + 1), V(zm, 0, P + 1), SIGN, best)
        turn(V("r1", 0, 32), V("bs", 64, 96))
        turn(V("r1", 32, 64, 1, 0, 64), V("bs", 64, 96, 1, 64, 128))
        turn(V("r1", 32, 64, 1, 64, 128), V("bs", 64, 96, 1, 0, 64))
        for a in range(4):
            b = a ^ 1
            act(V("dd", 32, 96, 1, 32 * a, 32 * a + 32), V("r1", 0, 64, 1, 32 * b, 32 * b + 32), SAME, part(best, 32 * a, 32 * a + 32))
        act(V("dd", 0, 32), V("r1", 0, 32), SAME, best)
        issue("s", lambda e, ib=ib, best=best: e.activation(ap(ib), ap(best), RELU, scale=-0.25 / BIG), [ib], [best])
        for b in range(3):
            keep(b, c)
        tt(V("kp", 0, P + 1), V(ky, M, KEYW, SEG), V("pen", 0, P + 1), A.subtract)
        ts(V("ca", 33, 65), V("r1", 32, 64), best, A.subtract, V("tl", 0, 1), A.is_ge)
        scan(V("cb", 0, 65), V("kp", 0, 65), V("kp", 64, 129), -2.0, A.max, A.max)
        ts(V("cb", 65, 129), V("dd", 32, 96), V("tl", 1, 2), A.is_le)
        tt(V("ca", 1, 33), V("dd", 0, 32), V("th", 0, 32), A.is_le)
        scan(V("u1", 0, 97), V("ca", 0, 97), V("cb", 64, 161), V("pc", h, h + 1), A.add, A.add)
        u1 = V("u1", 64, 65)
        turn(V("r2", 0, 32), V("u1", 65, 97))
        turn(V("r2", 32, 64, 1, 0, 64), V("u1", 65, 97, 1, 64, 128))
        turn(V("r2", 32, 64, 1, 64, 128), V("u1", 65, 97, 1, 0, 64))
        for a in range(4):
            b = a ^ 1
            cp("vsvs"[a], V("r2", 64, 128, 1, 32 * a, 32 * a + 32), V("r2", 0, 64, 1, 32 * b, 32 * b + 32))
        keep(3, c)
        won = V("sm", 5, 6)
        red(won, V("r2", 0, P), A.min, True)
        ts(hi4, V("c4", 4 * h, 4 * h + 4), won, A.add, 512.0, A.mult)
        ts(V("sm", 6, 7), won, 1.5 * 2 ** 12, A.add, 1.5 * 2 ** 12, A.subtract)
        if not last:
            cp("v", V("si%d" % (t + 1), 0, K), V("idtab", 0, 2 * P), hi)
            post_ids(t + 1)
            ts(lo, won, V("sm", 6, 7), A.subtract, 1.0 / UNIT, A.mult)
        else:
            ts(V("sm", 3, 4), won, 1.0 / UNIT, A.mult, 192.0, A.add)
            tt(V("val", 0, K), V("dm", 0, 2 * P), V("vr", 0, K), A.mult, hi)
            ts(lo, V("sm", 6, 7), -1.0 / UNIT, A.mult, V("sm", 3, 4), A.add)
        for b in range(4):
            cp("s", V("go", K * b, K * b + K), V("dec", 512 * b, 512 * b + 2 * P), hi)
        for b in range(4):
            tt(V("ht", b, 4 * K, 4), V("dec", 512 * b + P, 512 * b + P * (t + 2)), V("go", K * b, K * b + K), A.add, lo)
        if last:
            scatter(V("mp", 0, 2 * P), V("val", 0, K), hi)
        quant(V("qa", c, c + P), V("sa", c, c + P), V("ht", 0, 512))
        if not last:
            post_cols(t + 1, "qa", "sa", c)
            pick(V("lq%d" % (t + 1), s0, s1), V("ls%d" % (t + 1), s0, s1), V("qa", c, c + P), V("sa", c, c + P), V("oid", 0, 1))
            if t == 1:
                quant(V("qw", 0, P * O), V("sw", 0, P * O), V("wt", 0, 512 * O))
                products_w(0)
                for o in range(O):
                    cp("s", V("yw", 2 * P * o, 2 * P * o + P), V("yb", 512 * o, 512 * o + P))
                new_y(0)
                new_y(1)
            cp("v", V("li%d" % (t + 1), s0, s1), V("si%d" % (t + 1), 0, K))
            ts(V("e5", 0, SEG * P, SEG), row, float(c) - 1472.0, A.add, UNIT, A.mult)
            ts(V("sm", 7, 8), ib, 100.0, A.mult, u1, A.add)
            fill(V(zn, P + 1, P + 32), -BIG)
            ts(V("sm", 8, 9), V("sm", 7, 8), float(K), A.is_lt, 8.0, A.mult)
            cp("v", V(kn, KEYW - 1, KEYW), km)
            tt(V("thr", 0, 1), V("thr", 0, 1), V("sm", 8, 9), A.add)
            cp("v", V("lif", P * t, P * t + P), li)
            ts(V("sm", 9, 10), V("thr", 0, 1), 1.0, A.is_lt, 2.0 * BIG, A.mult)
            ts(V("vr", 0, K), V("row", 0, K), float(c), A.add)
            ts(V(zn, P, P + 1), V("sm", 9, 10), -BIG, A.add, best, A.min)
            if t == 0:
                late_constants()
            cp("s", V(yn, K * O, K * O + K), V("lif", 0, c), lo)
            tt(V("val", 0, K), V("dm", 0, 2 * P), V("vr", 0, K), A.mult, hi)
            scatter(V("mp", 0, 2 * P), V("val", 0, K), hi)
            if t == 1:
                ts(V("vr", 0, K), V("row", 0, K), float(c + P), A.add)
                for u in range(2):
                    scatter(V("yw", 0, pw + 2 * P), V("yn%d" % u, 0, K * O + K), V("of%d" % u, 0, 4))
        else:
            cp("s", V(yn, K * O, K * O + K), V("lif", 0, c), lo)
            new_y(t)
            scan(V("mps", 0, P), V("rst16", 0, P), V("mp", 0, P), 0.0)
            cp("v", V("omap", 0, 8), V("mps", 15, P, 16))
            for o in range(O):
                scatter(V("yw", 2 * P * o, 2 * P * o + 2 * P), V(yn, K * o, K * o + K), hi)
                dma("y", "d_out", T.y[:, P * o:P * o + P], T.yw[:, 2 * P * o:2 * P * o + P], [], [V("yw", 2 * P * o, 2 * P * o + P)])
            pick(V("qf", 0, P), V("sf", 0, P), V("qa", 0, 512), V("sa", 0, 512), V("omap", 0, 8))
            dma("y", "d_out", T.oc[:], T.qf[:, 0:P].bitcast(dt.uint8), [], [V("qf", 0, P)])
            scatter(V("yw", pw, pw + 2 * P), V(yn, K * O, K * O + K), hi)
            for a in range(4):
                dma("s", "d_out", T.osc[4 * a:4 * a + 4, 0:P], T.sf[32 * a:32 * a + 4, 0:P], [], [V("sf", 0, P)])
            dma("y", "d_out", T.pa[:], T.yw[0:1, pw:pw + P], [], [V("yw", pw, pw + P)])

    value = {}
    run = {q: 0 for q in eng}
    for q, call, waits, tok, sem in ops:
        if sem is None and tok in waited:
            run[q] += 1
            value[tok] = run[q]
    for q, call, waits, tok, sem in ops:
        for w in waits:
            if w in value:
                eng[q].wait_ge(T.sem["c_" + w[0]], value[w])
            else:
                eng[q].wait_ge(T.sem[w[0]], total[w[0]])
        ins = call(eng[q])
        if sem is not None:
            ins.then_inc(T.sem[sem], 16)
        elif tok in value:
            ins.then_inc(T.sem["c_" + q], 1)
    g.wait_ge(T.sem.gone, sent[0])
    g.sync.wait_ge(T.sem.d_out, total["d_out"])
